import numpy as np, ml_dtypes
CORES = [1,5,17,21,33,37,49,53]
N = 8
BF = ml_dtypes.bfloat16
def gentries(a):
    return np.ascontiguousarray(a.reshape(8, 16, -1).transpose(0, 2, 1)).reshape(8, -1)
def gtable(e):
    e = np.asarray(e); return np.ascontiguousarray(e.reshape(8, -1, 16).transpose(0, 2, 1)).reshape(128, -1).astype(np.int32)
ND, NR, L, CAP, HB, LV, RO = 2048, 4096, 256, 32, 1, 3, 2
def parts(rng):
    cold = rng.random((N, 8, 1, NR)) < 0.4; cold[..., 5] = True
    regs = rng.integers(-15, 16, (N, 8, 16, NR)); warm = rng.random(regs.shape) < rng.random((N, 8, 1, NR))
    regs = np.where(cold | ~warm, -np.abs(regs), regs)
    acts = rng.integers(0, NR, (N, 8, 16, ND)); dead = rng.random((N, 8, 1, ND)) < 0.125
    order = np.argsort(~cold[:, :, 0], axis=-1, kind="stable"); cnt = np.add.reduce(cold[:, :, 0].astype(np.int64), axis=-1)
    pick = (rng.random(acts.shape) * cnt[:, :, None, None]).astype(np.int64).reshape(N, 8, -1)
    acts = np.where(dead, np.take_along_axis(order, pick, 2).reshape(acts.shape), acts)
    return acts, regs, rng.integers(0, 16, (N, 8, 16, ND)), rng.integers(0, ND, (N, 8, L)), rng.integers(1, 16, (N, 8, 16, L)), rng.integers(0, 64, (N, 8, RO, LV, L))
def pack(acts, regs, pay, n0, rch, dr):
    b = lambda a: np.ascontiguousarray(a.reshape(N, 128, -1)).astype(np.float32).astype(BF)
    return {"acts": np.ascontiguousarray(acts.reshape(N, 128, ND)).astype(np.int32), "regs": b(regs), "pay": b(pay), "n0": np.stack([gtable(a) for a in n0]), "rch": b(rch),
            "dr": np.ascontiguousarray(dr.reshape(N, 8, RO * LV * L)).astype(np.int32)}
def setup_inputs(rng):
    return pack(*parts(rng))
def setup_inputs_room(rng):
    acts, regs, pay, n0, rch, dr = parts(rng)
    regs[:, ::2] = -rng.integers(2 * RO, 16, (N, 4, 16, NR)); pay = pay * rng.integers(0, 2, pay.shape)
    for q in range(N):
        for g in range(0, 8, 2):
            for t in range(RO):
                p = int(rng.integers(0, 4))
                if q == 0: p = (g // 2 + (t if g else 0)) % 4
                c = np.zeros(N, np.int64)
                if p == 0: c[:] = CAP
                elif p == 1: c[::2] = CAP + 1; c[1::2] = CAP - 1
                elif p == 2: c[0] = L
                else: c[1] = 1; c[2] = CAP; c[3] = L - 1 - CAP
                to = rng.permutation(np.repeat(np.arange(N), np.roll(c, int(rng.integers(0, N)))))
                dr[q, g, t, HB - 1] = to + N * rng.integers(0, 64 // N, L)
    return pack(acts, regs, pay, n0, rch, dr)
def setup_inputs_ties(rng):
    acts, regs, pay, n0, rch, dr = parts(rng)
    for g in (0, 3, 6):
        regs[:, g] = 15; rch[:, g] = rng.integers(1, 16 - 2 * RO, (N, 16, L))
        dr[:, g] = rng.choice(np.concatenate([4 * np.arange(16), 4 * np.arange(1, 16) - 1, np.array([63])]), (N, RO, LV, L))
    for g in (1, 4):
        i = rng.integers(0, 16, (N, 1, NR)); one = (np.arange(16)[None, :, None] == i) & (rng.random((N, 1, NR)) < 0.25)
        regs[:, g] = np.where(one, 1, -rng.integers(0, 16, (N, 16, NR)))
        dr[:, g] = 8 * rng.integers(0, 8, (N, RO, LV, L))
    for g in (2, 5, 7):
        dr[:, g] = rng.choice(np.array([0, 1, 31, 32, 62, 63]), (N, RO, LV, L))
    return pack(acts, regs, pay, n0, rch, dr)
def setup_inputs_alike(rng):
    acts, regs, pay, n0, rch, dr = parts(rng)
    n0[:, ::2] = rng.choice(np.array([0, ND - 1, ND // 2, 3]), (N, 4, L))
    acts[:, 1] = rng.choice(np.array([0, NR - 1, 7, NR // 2]), (N, 16, ND))
    acts[:, 5] = rng.integers(NR - 64, NR, (N, 16, ND)); acts[:, 7] = rng.integers(0, 100, (N, 16, ND))
    acts[:, 2] = acts[:, 2, :1]
    dr[:, 4:] = dr[:, 4:, :, :, :1]
    return pack(acts, regs, pay, n0, rch, dr)
def setup_inputs_clip(rng):
    acts, regs, pay, n0, rch, dr = parts(rng)
    regs = rng.choice(np.array([-15, -14, -1, 0, 1, 14, 15]), (N, 8, 16, NR)); pay = 15 * rng.integers(0, 2, pay.shape)
    rch = np.where(rng.random(rch.shape) < 0.7, 15, rng.integers(1, 3, rch.shape))
    a, b = rng.permutation(8)[:2]
    regs[:, a] = 15; rch[:, a] = 15; regs[:, b] = -15
    return pack(acts, regs, pay, n0, rch, dr)
def setup_inputs_spread(rng):
    acts, regs, pay, n0, rch, dr = parts(rng)
    u = lambda shape: np.minimum((np.exp2(4 * rng.random((N, 8, 1, shape[-1]))) * rng.random(shape)).astype(np.int64), 15)
    regs = u(regs.shape) * np.where(rng.random(regs.shape) < rng.random((N, 8, 1, NR)), 1, -1)
    pay = u(pay.shape); rch = np.maximum(u(rch.shape), 1)
    dr = np.minimum((64 * rng.random(dr.shape) ** np.exp2(4 * rng.random((N, 8, 1, 1, L)) - 2)).astype(np.int64), 63)
    return pack(acts, regs, pay, n0, rch, dr)
def check_inputs(d):
    bad = []
    for k, lo, hi in (("acts", 0, NR - 1), ("regs", -15, 15), ("pay", 0, 15), ("n0", 0, ND - 1), ("rch", 1, 15), ("dr", 0, 63)):
        a = np.asarray(d[k]).astype(np.float64)
        if not (np.min(a) >= lo and np.max(a) <= hi): bad.append("range of " + k)
        elif not np.all(a == np.rint(a)): bad.append("whole numbers in " + k)
    return bad
def level(rg, ac, n, x, v, e):
    S = n.shape[1]
    a = np.take_along_axis(ac, n[:, None, :], 2)
    p = np.maximum(np.take_along_axis(rg, a.reshape(8, 1, 16 * S), 2), 0).reshape(8, 16, 16, S)
    c = np.add.accumulate(np.add.reduce(np.minimum(x[:, :, None, :], p), axis=1), axis=1)
    tot = c[:, 15]
    k = np.where(tot > 0, np.argmax(64 * c > (v * tot)[:, None, :], axis=1), v & 15)
    rec = np.take_along_axis(a, k[:, None, :], 1)[:, 0]
    x = np.minimum(x, np.take_along_axis(p, k[:, None, None, :], 2)[:, :, 0] + 1)
    return k, rec, x, (5 * rec + 13 * n + e) & (ND - 1)
def rewrite(rg, rec, live, w):
    for g in range(8):
        s = np.nonzero(live[g])[0]
        u, j = np.unique(rec[g, s], return_index=True)
        rg[g][:, u] = np.clip(rg[g][:, u] + w[g][:, s[j]], -15, 15)
def reference(acts, regs, pay, n0, rch, dr):
    ac = acts.astype(np.int64).reshape(N, 8, 16, ND); rg = regs.astype(np.float32).astype(np.int64).reshape(N, 8, 16, NR)
    py = pay.astype(np.float32).astype(np.int64).reshape(N, 8, 16, ND); x0 = rch.astype(np.float32).astype(np.int64).reshape(N, 8, 16, L)
    st = np.stack([gentries(a) for a in n0]).astype(np.int64); v = dr.astype(np.int64).reshape(N, 8, RO, LV, L)
    for t in range(RO):
        fn = np.zeros((N, 8, N * CAP), np.int64); fx = np.ones((N, 8, 16, N * CAP), np.int64); fv = np.zeros((N, 8, LV, N * CAP), np.int64); live = np.zeros((N, 8, N * CAP), bool)
        home = []
        for r in range(N):
            n, x, vt = st[r], x0[r], v[r, :, t]
            for e in range(1, HB + 1): k, rec, x, n = level(rg[r], ac[r], n, x, vt[:, e - 1], e)
            to = k & (N - 1); oh = (to[:, None, :] == np.arange(N)[None, :, None]).astype(np.int64)
            place = np.take_along_axis(np.add.accumulate(oh, axis=2), to[:, None, :], 1)[:, 0] - 1
            g, l = np.nonzero(place < CAP); d = to[g, l]; s = r * CAP + place[g, l]
            fn[d, g, s] = n[g, l]; fx[d, g, :, s] = x[g, :, l]; fv[d, g, :, s] = vt[g, :, l]; live[d, g, s] = True
            home.append((rec, g, l, d, s))
        recs, sg = [], []
        for q in range(N):
            n, x = fn[q], fx[q]
            for e in range(HB + 1, LV + 1): k, rec, x, n = level(rg[q], ac[q], n, x, fv[q, :, e - 1], e)
            val = np.minimum(np.take_along_axis(py[q], n[:, None, :], 2), x)
            recs.append(rec); sg.append(np.sign(16 * val - np.add.reduce(val, axis=1, keepdims=True)))
        for q in range(N): rewrite(rg[q], recs[q], live[q], sg[q])
        sg = np.stack(sg)
        for r in range(N):
            rec, g, l, d, s = home[r]
            w = np.zeros((8, 16, L), np.int64); went = np.zeros((8, L), bool)
            w[g, :, l] = -sg[d, g, :, s]; went[g, l] = True
            rewrite(rg[r], rec, went, w)
    return {"yr": rg.reshape(N, 128, NR).astype(np.float32).astype(BF)}

@@ -1,0 +1,549 @@
+from concourse.bass import DstId, RemoteDMATransfer
+from concourse.mybir import AluOpType as A, ActivationFunctionType as F
+
+ETA, DEL = 2.0 ** -24, 2.0 ** -12
+N, ND, NR, RO = 8, 2048, 4096, 2
+DT = {"F": "float32", "B": "bfloat16", "H": "float16", "I": "int32", "U": "uint16"}
+BIG = ("ACT I 2048;REG B 4352;PAYT B 2048;BT F 2048;T5 I 2048;T12 I 2048;n0i I 16;XR B 256;VI I 512;LC B 2048;SelN H 2048;LP B 2048;LT H 2048;P B 4096;"
+       "MN B 4096;E H 4096;W0 B 4096;W1 B 4096;LAND0 B 512;LAND1 B 512;NZ0 B 256;NZ1 B 256;ZL0 B 256;ZL1 B 256")
+SMALL = ("VI15 I 512;HPv B 512;HP15 B 512;KBr B 128;KBa B 128;KB B 128;pI I 8;pA I 8;pc F 16;JI F 16;JU U 16;I16 F 16;LTC F 16;LM F 256;DIAGN F 256;BO B 128;"
+         "BOx B 128;BOw B 128;BOn H 128;BOf H 128;EM H 128;SelNb B 256;D H 128;D2 H 128;t1 F 128;t2 F 128;t3 F 128;t4 F 128;t5 F 128;t6 F 128;m8 F 128;d2a F 128;d2b F 128;"
+         "d2c F 128;IDh H 128;IDb B 128;SHb B 128;RV B 384;RW B 384;CWa F 128;CWb F 128;CW B 128;ZMa F 128;ZM B 128;ONES B 128;ZF F 128;ZB B 256;TRASH F 16;ADDK H 8;"
+         "NU0 U 16;A1 U 256;G5 I 256;G12 I 256;Bg1 F 256;bhI I 256;blI I 256;bh B 256;bl B 256;nA I 16;nB I 16;nC I 16;nD I 16;Nh F 16;Nl F 16;NMXh B 256;NMXl B 256;"
+         "A16 U 256;Bg F 256;V1 F 512;CM H 256;Tt F 256;Q H 512;Pk B 256;ADDL H 32;LI I 32;L2 I 32;LU U 128;NI I 16;NN I 16;Na I 16;Nb I 16;LIVE F 16;CNT F 256;QC H 256;"
+         "SL U 32;KU U 16;OFF I 16;ph B 256;pl B 256;SC B 512;oa I 16;ob I 16;oc I 16;od I 16;oe I 16;ZIX U 16;GO F 16;KI I 16;KJ I 16;AI I 32;AU U 32;KBs H 256;dead F 16;"
+         "KM F 16;KL F 16;DPs H 256;w1 F 16;w2 F 16;w3 F 16;w4 F 16;w5 F 16;OW U 32;XS B 256;VAL B 256;NEW B 256;NEWc B 256;OLD B 256")
+SCRATCH, WHERE, _fill = {}, {}, {}
+for _x in BIG.split(";"):
+    _n, _d, _w = _x.split()
+    SCRATCH[_n] = ("sbuf", [128, int(_w)], DT[_d])
+    WHERE[_n] = (_n, 0, int(_w))
+for _x in SMALL.split(";"):
+    _n, _d, _w = _x.split()
+    WHERE[_n] = ("pool" + _d, _fill.get(_d, 0), int(_w))
+    _fill[_d] = _fill.get(_d, 0) + (int(_w) + 15) // 16 * 16
+for _d in _fill:
+    SCRATCH["pool" + _d] = ("sbuf", [128, _fill[_d]], DT[_d])
+for _i in range(8):
+    SCRATCH["ps%d" % _i] = ("psum", [128, 512], "float32")
+    WHERE["ps%d" % _i] = ("ps%d" % _i, 0, 512)
+SEMAPHORES = ["qV", "qS", "qT", "qG", "loc", "ldn0", "ldacts", "ldregs", "ldpay", "ldrch", "lddr", "st"]
+for _t in range(RO):
+    SEMAPHORES += ["hA%d" % _t, "hB%d" % _t, "zA%d" % _t, "zB%d" % _t]
+
+
+def plan(q, cores, topo):
+    out = []
+    mine = q // 4
+    for half in (mine, 1 - mine):
+        rs = [r for r in range(4 * half, 4 * half + 4) if r != q]
+        far = [r for r in rs if topo.chip(cores[r]) != topo.chip(cores[q])]
+        near = [r for r in rs if r not in far]
+        call, used = [], []
+        for grp in (far, near):
+            for i, r in enumerate(grp):
+                e = [x for x in topo.engines(cores[q], cores[r]) if grp is far or x not in used]
+                n = len(e) // len(grp)
+                call.append((r, e[i * n:(i + 1) * n]))
+            used = [x for _, e in call for x in e]
+        out.append(call)
+    return out
+
+
+def rank_program(g, core, T, topo):
+    q = T.rank_of(core)
+    if q is None:
+        return
+    cores = list(T.cores)
+    eng = {"V": g.vector, "S": g.scalar, "T": g.tensor, "G": g, "Y": g.sync}
+    clk = {k: {} for k in eng}
+    cnt = {"V": 0, "S": 0, "T": 0, "G": 0}
+    acc = {}
+    banks = {}
+
+    def v(name, a=0, b=None, st=1):
+        buf, off, w = WHERE[name]
+        return (buf, off + a, off + (w if b is None else b), st)
+
+    def ap(x):
+        return T[x[0]][:, x[1]:x[2]] if x[3] == 1 else T[x[0]][:, x[1]:x[2]:x[3]]
+
+    def meet(x, y):
+        if x[2] <= y[0] or y[1] <= x[1]:
+            return False
+        return not (x[3] == y[2] and x[3] > 1 and (x[1] - y[0]) % x[3])
+
+    def need(qn, evs):
+        best = {}
+        for e in evs:
+            if clk[qn].get(e[0], 0) < e[1] and (e[0] not in best or best[e[0]][1] < e[1]):
+                best[e[0]] = e
+        lst = list(best.values())
+        keep = [e for e in lst if not any(o is not e and o[2].get(e[0], 0) >= e[1] for o in lst)]
+        for e in keep:
+            eng[qn].wait_ge(T.sem[e[0]], e[1])
+        for e in keep:
+            for k, x in list(e[2].items()) + [(e[0], e[1])]:
+                if clk[qn].get(k, 0) < x:
+                    clk[qn][k] = x
+
+    def deps(qn, reads, writes):
+        evs = []
+        for lst, wr in ((reads, False), (writes, True)):
+            for x in lst:
+                evs += [e for k, e in banks.get(x[0], {}).items() if k != qn]
+                for y in acc.get(x[0], []):
+                    if meet(x, y) and (y[3] or wr) and not qn == y[4] == "T":
+                        evs.append(y[5])
+        return evs
+
+    def note(qn, reads, writes, ev):
+        for lst, wr in ((reads, False), (writes, True)):
+            for x in lst:
+                if x[0].startswith("ps"):
+                    banks.setdefault(x[0], {})[qn] = ev
+                l = acc.setdefault(x[0], [])
+                if wr and x[3] == 1:
+                    l[:] = [y for y in l if not (x[1] <= y[0] and y[1] <= x[2])]
+                elif not wr:
+                    l[:] = [y for y in l if not (y[:3] == x[1:] and not y[3] and y[4] == qn)]
+                l.append((x[1], x[2], x[3], wr, qn, ev))
+
+    def op(qn, fn, reads, writes):
+        need(qn, deps(qn, reads, writes))
+        cnt[qn] += 1
+        fn().then_inc(T.sem["q" + qn], 1)
+        note(qn, reads, writes, ("q" + qn, cnt[qn], dict(clk[qn])))
+
+    def dma(qn, out, in_, sem, reads=(), writes=()):
+        need(qn, deps(qn, reads, writes))
+        eng[qn].dma_start(out, in_).then_inc(T.sem[sem], 16)
+        note(sem, reads, writes, (sem, 16, dict(clk[qn])))
+
+    def tt(out, a, b, o):
+        op("V", lambda: g.vector.tensor_tensor(ap(out), ap(a), ap(b), o), [a, b], [out])
+
+    def ttg(out, win, off, b, o):
+        op("V", lambda: g.vector.tensor_tensor(ap(out), ap(win).indirect(ap(off)), ap(b), o), [win, off, b], [out])
+
+    def ts(out, a, s1, o1, s2=None, o2=None):
+        rd = [a] + [s for s in (s1, s2) if isinstance(s, tuple)]
+        s = [ap(x) if isinstance(x, tuple) else x for x in (s1, s2)]
+        if o2 is None:
+            op("V", lambda: g.vector.tensor_scalar(ap(out), ap(a), s[0], None, o1), rd, [out])
+        else:
+            op("V", lambda: g.vector.tensor_scalar(ap(out), ap(a), s[0], s[1], o1, o2), rd, [out])
+
+    def cp(out, a):
+        op("V", lambda: g.vector.tensor_copy(ap(out), ap(a)), [a], [out])
+
+    def cpg(out, win, off):
+        op("V", lambda: g.vector.tensor_copy(ap(out), ap(win).indirect(ap(off))), [win, off], [out])
+
+    def scat(win, off, a):
+        op("V", lambda: g.vector.tensor_copy(ap(win).indirect(ap(off)), ap(a)), [off, a], [win])
+
+    def fill(out, c):
+        op("V", lambda: g.vector.memset(ap(out), c), [], [out])
+
+    def act(out, a, fn, off=None, **kw):
+        if off is None:
+            op("S", lambda: g.scalar.activation(ap(out), ap(a), fn, **kw), [a], [out])
+        else:
+            op("S", lambda: g.scalar.activation(ap(out), ap(a).indirect(ap(off)), fn, **kw), [a, off], [out])
+
+    def mm(out, l, r, start, stop):
+        op("T", lambda: g.tensor.matmul(ap(out), ap(l), ap(r), start, stop), [l, r], [out])
+
+    def B(name, j, w=128):
+        return v(name, w * j, w * j + w)
+
+    dma("Y", T.n0i[:, :], T.n0[:, :], "ldn0", [], [v("n0i")])
+    dma("Y", T.ACT[:, :], T.acts[:, :], "ldacts", [], [v("ACT")])
+    dma("Y", T.REG[:, 0:NR], T.regs[:, :], "ldregs", [], [v("REG", 0, NR)])
+    dma("Y", T.PAYT[:, :], T.pay[:, :], "ldpay", [], [v("PAYT")])
+    dma("S", T.XR[:, :], T.rch[:, :], "ldrch", [], [v("XR")])
+    fill(v("VI"), 0)
+    need("S", [("qV", cnt["V"], {})])
+    for t in range(RO):
+        for e, row in ((1, 6), (2, 2), (3, 4)):
+            c = (t * 3 + e - 1) * 256
+            g.scalar.dma_start(T.VI[row::16, t * 256:t * 256 + 256], T.dr[:, c:c + 256]).then_inc(T.sem["lddr"], 16)
+    note("lddr", [], [v("VI")], ("lddr", 96, dict(clk["S"])))
+
+    def iota(name, pattern, cm, **kw):
+        op("G", lambda: g.iota(ap(v(name)), pattern, 0, cm, **kw), [], [v(name)])
+
+    def aff(out, a, pattern, cmp, fillv, base, cm):
+        op("G", lambda: g.affine_select(ap(out), ap(a), pattern, cmp, fillv, base, cm), [a], [out])
+    some = {"allow_small_or_imprecise_dtypes": True}
+    iota("KBr", [[0, 8], [1, 16]], 0, **some)
+    aff(v("KBa"), v("KBr"), [[-16, 8], [0, 16]], A.is_ge, -100.0, 0, 1)
+    aff(v("KB"), v("KBa"), [[16, 8], [0, 16]], A.is_ge, -100.0, 15, -1)
+    iota("pI", [[0, 8]], 1)
+    iota("JI", [[1, 16]], 0, **some)
+    iota("LM", [[0, 16], [1, 16]], 0, **some)
+    fill(v("ONES"), 1.0)
+    fill(v("ZF"), 0.0)
+    fill(v("ZB"), 0.0)
+    for d in range(N):
+        fill(v("W0", 512 * d, 512 * d + 64), 0.0)
+    ts(v("pA"), v("pI"), 15, A.bitwise_and)
+    pc = [v("pc", i, i + 1) for i in range(9)]
+    cp(pc[0], v("pA", 0, 1))
+    cp(v("JU"), v("JI"))
+    for i, m, a in ((1, 1, 1), (2, 1, -7), (3, 1, -8), (4, -256, 1), (5, 16, -2032), (6, 1, 4096)):
+        ts(pc[i], pc[0], float(m), A.mult, float(a), A.add)
+    KB, JI = v("KB"), v("JI")
+    ts(v("I16"), JI, pc[0], A.is_equal)
+    ts(v("LTC"), JI, pc[0], A.is_gt)
+    ts(v("BO"), KB, 0.0, A.is_ge)
+    ts(v("t6"), KB, 15.0, A.is_equal)
+    ts(pc[7], v("I16", 0, 1), 64.0, A.mult, v("I16", 1, 2), A.add)
+    tt(pc[8], v("I16", 7, 8), v("I16", 15, 16), A.add)
+    tt(v("BOx"), v("BO"), v("t6"), A.subtract)
+    ts(v("BOw"), v("BO"), pc[7], A.mult)
+    for k in range(16):
+        aff(B("LC", k), v("BOx") if k < 8 else v("BO"), [[0, 8], [1, 16]], A.is_ge, 0.0, -k, 0)
+    for j in range(16):
+        aff(B("LP", j), v("BOw"), [[0, 8], [1, 16]], A.is_equal, 0.0, -j, 0)
+    ts(v("EM"), v("BO"), pc[8], A.mult)
+    ts(v("DIAGN"), v("LM"), pc[0], A.is_equal, -1.0, A.mult)
+    ts(v("TRASH"), JI, 16.0, A.mult, pc[6], A.add)
+    ts(v("ADDK"), v("JI", 0, 8), 256.0, A.mult, pc[5], A.add)
+    ts(v("BOn"), KB, 0.0, A.is_ge, -1.0, A.mult)
+    ts(v("BOf"), KB, 0.0, A.is_ge)
+    for i, r in enumerate((6, 2, 4)):
+        ts(B("RV", i), v("BO"), v("I16", r, r + 1), A.mult)
+    for i, r in enumerate((6, 3, 5)):
+        ts(B("RW", i), v("BO"), v("I16", r, r + 1), A.mult, ETA, A.mult)
+    ts(v("CWa"), KB, 0.5, A.add, -ETA, A.mult)
+    ts(v("m8"), v("t6"), -16384.0, A.mult)
+    ts(v("t5"), v("BO"), v("I16", 0, 1), A.mult)
+    tt(v("CWb"), v("CWa"), v("m8"), A.add)
+    ts(v("t1"), KB, pc[1], A.is_equal)
+    ts(v("t2"), KB, pc[0], A.is_equal)
+    ts(v("t3"), KB, pc[2], A.is_equal)
+    ts(v("t4"), KB, pc[3], A.is_equal)
+    tt(v("CW"), v("CWb"), v("t5"), A.mult)
+    tt(v("D"), v("t1"), v("t2"), A.subtract)
+    tt(v("d2a"), v("t1"), v("t2"), A.subtract)
+    tt(v("d2b"), v("t3"), v("t4"), A.subtract)
+    ts(v("m8"), KB, 8.0, A.is_lt)
+    tt(v("d2c"), v("d2a"), v("d2b"), A.add)
+    cp(v("NU0"), v("n0i"))
+    cp(v("IDh"), v("t2"))
+    tt(v("D2"), v("d2c"), v("m8"), A.mult)
+    cp(v("IDb"), v("t2"))
+    cp(v("SHb"), v("t1"))
+    for j in range(16):
+        ts(B("SelN", j), KB, float(j), A.is_equal, -1.0, A.mult)
+    for j in range(2):
+        ts(B("SelNb", j), KB, float(j), A.is_equal, -1.0, A.mult)
+    for h in range(2):
+        cpg(B("A1", h), v("ACT"), B("NU0", h, 8))
+    ts(v("nA"), v("n0i"), 13.0, A.mult, 1.0, A.add)
+    ts(v("G5"), v("A1"), 5.0, A.mult)
+    ts(v("nB"), v("nA"), ND - 1, A.bitwise_and)
+    ts(v("G12"), v("G5"), 4095, A.bitwise_and)
+    ts(v("nC"), v("nB"), 6, A.logical_shift_right)
+    ts(v("nD"), v("nB"), 63, A.bitwise_and)
+    ts(v("bhI"), v("G5"), 6, A.logical_shift_right, 31, A.bitwise_and)
+    ts(v("Nh"), v("nC"), 64.0, A.add)
+    cp(v("Nl"), v("nD"))
+    ts(v("blI"), v("G5"), 63, A.bitwise_and)
+    cp(v("bh"), v("bhI"))
+    ttg(v("NMXh"), v("Nh"), v("JU"), v("DIAGN"), A.mult)
+    ttg(v("NMXl"), v("Nl"), v("JU"), v("DIAGN"), A.mult)
+    cp(v("bl"), v("blI"))
+    cp(v("ps0", 256, 512), v("XR"))
+    ts(v("VI15"), v("VI"), 15, A.bitwise_and)
+    cp(v("HPv"), v("VI"))
+    cp(v("HP15"), v("VI15"))
+    ts(v("T5"), v("ACT"), 5.0, A.mult)
+    ts(v("T12"), v("T5"), 4095, A.bitwise_and)
+
+    def later_constants():
+        ts(v("BT"), v("T12"), -2048.0, A.add)
+        ts(v("ZMa"), v("t2"), 16.0, A.mult)
+        for h in range(2):
+            cp(B("ADDL", 2 * h + 1, 8), v("ADDK"))
+        tt(v("ZM"), v("ZMa"), v("BO"), A.subtract)
+        for d in range(N):
+            fill(v("W1", 512 * d, 512 * d + 64), 0.0)
+
+    def Cb(h):
+        return v("ps%d" % (1 + h), 0, 128)
+
+    def Mb(h, a=0, b=128):
+        return v("ps%d" % (3 + h), a, b)
+
+    recs = v("REG", 0, NR)
+
+    def minima(h, xcol, lev, draws15, ks=range(16)):
+        for k in ks:
+            mk = B("MN", 16 * h + k)
+            tt(mk, v("P", 2048 * h + k, 2048 * h + 2048, 16), v("ps0", xcol + 128 * h, xcol + 128 * h + 128), A.min)
+            if k == 0:
+                mm(Mb(h), v("CW"), v("ONES"), True, False)
+                mm(Mb(h), B("RW", lev - 1), draws15, False, False)
+            mm(Cb(h), B("LC", k), mk, k == 0, k == 15)
+
+    def decide(h, v1, gap=lambda: None):
+        cp(B("CM", h), Cb(h))
+        mm(Mb(h), v("EM"), B("CM", h), False, True)
+        gap()
+        tt(B("Tt", h), Mb(h), v1, A.mult)
+        tt(cond(h), Cb(h), B("Tt", h), A.is_gt)
+
+    def cond(h, j=None):
+        return B("Q", 2 * h + 1) if j is None else v("Q", 256 * h + 128 + j, 256 * h + 256, 16)
+
+    def chosen(h, lists):
+        act(B("Pk", h), B("P", h, 2048), F.Identity, off=lists, bias=1.0)
+
+    def thresholds(out, ps):
+        act(out, ps, F.Identity, scale=1.0 / 64, bias=DEL / 64)
+
+    sent = [0]
+    plans = [plan(r, cores, topo) for r in range(N)]
+    mine = q // 4
+    order = (mine, 1 - mine)
+
+    def send(src, dst, width, swidth, call, sem):
+        tr = []
+        for r, e in plans[q][call]:
+            rid, pid, _ = topo.addr(cores[r])
+            tr.append(RemoteDMATransfer(dst_ids=[DstId(rid=rid, pnc=pid)], dma_engine_mask=sum(1 << x for x in e), remote_sem=T.sem[sem],
+                                        srcs=[T[src][:, r * swidth:r * swidth + width]], dsts=[T[dst][:, q * width:q * width + width]]))
+            sent[0] += len(e)
+        g.remote_dma_fused(tr, local_sem=T.sem.loc)
+
+    def landed(buf, width, sems):
+        for i, h in enumerate(order):
+            val = sum(len(e) for r in range(N) if r != q for d, e in plans[r][i] if d == q)
+            for r in range(4 * h, 4 * h + 4):
+                if r != q:
+                    note(sems[i], [], [B(buf, r, width)], (sems[i], val, {}))
+
+    def sel(j):
+        return B("SelN", j)
+
+    def keys(h, live):
+        kl, KMh, KLh, dd = B("ps7", h, 8), B("KM", h, 8), B("KL", h, 8), B("dead", h, 8)
+        lv = (live[0], live[1] + 8 * h, live[1] + 8 * h + 8, 1)
+        mm(B("ps7", 1 + h), v("BOn"), B("Q", 2 * h), True, True)
+        for j in range(16):
+            mm(kl, sel(j), v("Q", 256 * h + j, 256 * h + 128, 16), j == 0, j == 15)
+        ts(dd, lv, -9999.0, A.mult, 9999.0, A.add)
+        cp(B("KBs", h), B("ps7", 1 + h))
+        tt(KMh, kl, lv, A.mult)
+        ts(B("KI", h, 8), kl, 2048.0, A.add)
+        tt(KLh, KMh, dd, A.add)
+
+    def matches(c, a, b):
+        e = lambda x: 240 * c + x
+        ts(v("E", e(a), e(b)), v("KBs", a, b), v("KL", c, c + 1), A.is_equal)
+        a = max(a, 16 * c + 16)
+        if a < b:
+            mm(v("ps6", 256 + a, 256 + b), v("BOf"), v("E", e(a), e(b)), False, False)
+
+    def inner(h, cs):
+        for c in cs:
+            matches(8 * h + c, 16 * (8 * h + c), 128 * h + 128)
+
+    def open_sums():
+        mm(v("ps6", 256, 512), v("BO"), v("ZB"), True, False)
+
+    def finish_sums(i, live):
+        for c in range(8):
+            matches(c, 128, 256)
+        for j in range(1, 16):
+            mm(v("ps6", 256 + j, 512, 16), B("LT", j), v("E", j, 4096, 256), False, j == 15)
+        ai = B("AI", i, 16)
+        ts(v("KJ"), v("KI"), 3277.0, A.mult)
+        ts(ai, v("KJ"), NR - 1, A.bitwise_and)
+        cp(B("AU", i, 16), ai)
+        tt(v("w3"), ai, v("TRASH"), A.subtract)
+        tt(v("w4"), v("w3"), live, A.mult)
+
+    def winners(i):
+        cp(v("DPs"), v("ps6", 256, 512))
+        for j in range(16):
+            mm(v("ps7", 32, 48), sel(j), v("DPs", j, 256, 16), j == 0, j == 15)
+        ts(v("w1"), v("ps7", 32, 48), 0.0, A.is_equal)
+        tt(v("w2"), v("w1"), v("w4"), A.mult)
+        tt(v("w5"), v("w2"), v("TRASH"), A.add)
+        cp(B("OW", i, 16), v("w5"))
+
+    def change(win, off, other, o, i):
+        ttg(v("NEW"), win, off, other, o)
+        ts(v("NEWc"), v("NEW"), 15.0, A.min, -15.0, A.max)
+        scat(v("REG"), B("OW", i, 16), v("NEWc"))
+
+    for t in range(RO):
+        W, LAND, NZ, ZL = "W%d" % t, "LAND%d" % t, "NZ%d" % t, "ZL%d" % t
+        for h in range(2):
+            act(B("P", h, 2048), recs, F.Relu, off=B("A1", h))
+            if h == 0:
+                mm(v("ps5", 0, 256), B("RV", 0), B("HPv", t, 256), True, True)
+                thresholds(v("V1", 0, 256), v("ps5", 0, 256))
+
+        def pay(h):
+            o = B("ps5", 2 + h)
+            mm(o, v("IDb"), B("HPv", 2 * t + h), True, False)
+            mm(o, v("SHb"), B("HP15", 2 * t + h), False, False)
+            for name, i in (("NMXh", 0), ("NMXl", 1), ("ph", 0), ("pl", 1)):
+                mm(o, B("SelNb", i), B(name, h), False, name == "pl")
+            act(B("SC", 2 * h + 1), o, F.Copy)
+
+        def places(h):
+            mm(Mb(h, 256, 384), v("D2"), cond(h), True, True)
+            mm(Mb(h, 128, 256), v("D"), cond(h), True, True)
+            init = pc[4] if h == 0 else v("CNT", 127, 128)
+            op("V", lambda: g.vector.tensor_tensor_scan(ap(B("CNT", h)), ap(Mb(h, 256, 384)), ap(v("ZF")), ap(init), A.add, A.add),
+               [Mb(h, 256, 384), v("ZF"), init], [B("CNT", h)])
+            tt(B("ph", h), Mb(h, 128, 256), B("bh", h), A.mult)
+            tt(B("QC", h), Mb(h, 256, 384), B("CNT", h), A.mult)
+            tt(B("pl", h), Mb(h, 128, 256), B("bl", h), A.mult)
+            for j in range(16):
+                mm(Mb(h, 400, 408), sel(j), v("QC", 128 * h + j, 128 * h + 128, 16), j == 0, j == 15)
+            mm(Mb(h, 384, 392), v("IDh"), v("ADDK"), True, False)
+            for j in range(16):
+                mm(Mb(h, 384, 392), sel(j), cond(h, j), False, j == 15)
+
+        def lists(h):
+            ts(B("KU", h, 8), Mb(h, 384, 392), 2048.0, A.add)
+            ts(B("SL", 2 * h + 1, 8), Mb(h, 400, 408), -2.0, A.mult, 1.0, A.add)
+            ts(B("SL", 2 * h, 8), Mb(h, 400, 408), -2.0, A.mult)
+            chosen(h, B("KU", h, 8))
+
+        def xpay(h):
+            tt(B("SC", 2 * h), B("ps0", 2 + h), B("Pk", h), A.min)
+
+        minima(0, 256, 1, B("HP15", 2 * t))
+        decide(0, B("V1", 0))
+        places(0)
+        pay(0)
+        minima(1, 256, 1, B("HP15", 2 * t + 1), range(8))
+        lists(0)
+        minima(1, 256, 1, B("HP15", 2 * t + 1), range(8, 16))
+        decide(1, B("V1", 1), lambda: xpay(0))
+        places(1)
+        pay(1)
+        scat(v(W), B("SL", 0, 16), B("SC", 0, 256))
+        lists(1)
+        scat(v(W), B("SL", 3, 8), B("SC", 3))
+        xpay(1)
+        scat(v(W), B("SL", 2, 8), B("SC", 2))
+        need("G", deps("G", [v(W)], []))
+        for i in range(2):
+            send(W, LAND, 64, 512, i, "h%s%d" % ("AB"[i], t))
+        for h in range(2):
+            tt(B("Q", 2 * h), Mb(h, 128, 256), B("Bg1", h), A.mult) if t else None
+        if t == 0:
+            ts(v("Bg1"), v("G12"), -2048.0, A.add)
+            for h in range(2):
+                tt(B("Q", 2 * h), Mb(h, 128, 256), B("Bg1", h), A.mult)
+        cp(B(LAND, q, 64), v(W, 512 * q, 512 * q + 64))
+        for h in range(2):
+            ts(B("OFF", h, 8), Mb(h, 400, 408), -1.0, A.mult)
+        ts(v("oc"), v("OFF"), 255, A.bitwise_and)
+        ts(v("oa"), v("OFF"), 8, A.logical_shift_right)
+        ts(v("ob"), v("OFF"), 31, A.bitwise_and)
+        ts(v("GO"), v("oc"), 32.0, A.is_lt)
+        ts(v("od"), v("oa"), 32.0, A.mult)
+        if t == 0:
+            for j in range(1, 16):
+                ts(B("LT", j), v("BO"), v("LTC", j, j + 1), A.mult)
+            later_constants()
+        tt(v("oe"), v("od"), v("ob"), A.add)
+        open_sums()
+        keys(0, v("GO"))
+        keys(1, v("GO"))
+        cp(v("ZIX"), v("oe"))
+        for h in range(2):
+            inner(h, range(8))
+        finish_sums(0, v("GO"))
+
+        landed(LAND, 64, ("hA%d" % t, "hB%d" % t))
+
+        def gathers(h, off):
+            cpg(B("A16", h), v("ACT"), off)
+            return lambda: (act(B("P", h, 2048), recs, F.Relu, off=B("A16", h)), act(B("Bg", h), v("BT"), F.Copy, off=off))
+
+        def nextn(h, node, lev):
+            ts(B("Na", h, 8), node, 13.0, A.mult, float(lev), A.add)
+            ts(B("Nb", h, 8), B("Na", h, 8), ND - 1, A.bitwise_and)
+            cp(B("ADDL", 2 * h, 8), B("Nb", h, 8))
+
+        def receive(h):
+            o, odd = Mb(h, 384, 392), v(LAND, 256 * h + 1, 256 * h + 256, 2)
+            for j in range(16):
+                mm(o, B("LP", j), v(LAND, 256 * h + 2 * j + 1, 256 * h + 256, 32), j == 0, j == 15)
+            ni, nn = B("NI", h, 8), B("NN", h, 8)
+            cp(ni, o)
+            ts(nn, ni, ND - 1, A.bitwise_and)
+            cp(B("LU", 8 * h, 8), nn)
+            gathers(h, B("LU", 8 * h, 8))()
+            for i in (0, 1):
+                mm(B("ps5", 2 * h + i), B("RV", 1 + i), odd, True, True)
+            thresholds(B("V1", h, 256), B("ps5", h, 256))
+            cp(B("ps0", h), v(LAND, 256 * h, 256 * h + 256, 2))
+            nextn(h, nn, 2)
+            ts(B("LIVE", h, 8), ni, 4096.0, A.is_ge)
+
+        def far(h, lev, gaps=()):
+            gaps = list(gaps) + [lambda: None] * 9
+            minima(h, 0, lev, v(LAND, 256 * h + 1, 256 * h + 256, 2))
+            decide(h, B("V1", 2 * h + lev - 2), gaps[0])
+            mm(Mb(h, 128, 256), v("D"), cond(h), True, True)
+            gaps[1]()
+            tt(B("Q", 2 * h), Mb(h, 128, 256), B("Bg", h), A.mult)
+            o = Mb(h, 384, 400)
+            mm(o, v("IDh"), B("ADDL", h, 16), True, False)
+            for j in range(16):
+                mm(o, sel(j), v("Q", 256 * h + j, 256 * h + 256, 16), False, j == 15)
+            gaps[2]()
+            ts(B("LI", h, 16), o, 2048.0, A.add)
+            ts(B("L2", h, 16), B("LI", h, 16), ND - 1, A.bitwise_and)
+            b = 64 * h + 16 * (lev - 1)
+            cp(v("LU", b, b + 16), B("L2", h, 16))
+            x, node = B("ps0", h), v("LU", b, b + 8)
+            later = gathers(h, node) if lev == 2 else None
+            chosen(h, v("LU", b + 8, b + 16))
+            if lev == 2:
+                later()
+                nextn(h, B("L2", 2 * h, 8), 3)
+                tt(x, x, B("Pk", h), A.min)
+            else:
+                gaps[3]()
+                tt(B("XS", h), x, B("Pk", h), A.min)
+                ttg(B("VAL", h), v("PAYT"), node, B("XS", h), A.min)
+                mm(Cb(h), v("ZM"), B("VAL", h), True, True)
+                act(B(NZ, h), Cb(h), F.Sign, scale=-1.0)
+                need("G", deps("G", [B(NZ, h)], []))
+                send(NZ, ZL, 32, 32, int(h != mine), "z%s%d" % ("AB"[int(h != mine)], t))
+
+        a, b = order
+        receive(a)
+        winners(0)
+        receive(b)
+        far(a, 2)
+        far(b, 2)
+        far(a, 3)
+        far(b, 3, (lambda: (open_sums(), keys(a, v("LIVE"))), lambda: inner(a, range(2)), lambda: inner(a, range(2, 8)), lambda: keys(b, v("LIVE"))))
+        inner(b, range(8))
+        finish_sums(1, v("LIVE"))
+        cp(B(ZL, q, 32), B(NZ, q, 32))
+        winners(1)
+        change(recs, B("AU", 1, 16), v(NZ), A.subtract, 1)
+        cpg(v("OLD"), recs, B("AU", 0, 16))
+        landed(ZL, 32, ("zA%d" % t, "zB%d" % t))
+        change(v(ZL), v("ZIX"), v("OLD"), A.add, 0)
+
+    dma("Y", T.yr[:, :], T.REG[:, 0:NR], "st", [recs], [])
+    g.sync.wait_ge(T.sem.st, 16)
+    for k in "VSTG":
+        need("Y", [("q" + k, cnt[k], {})])
+    g.wait_ge(T.sem.loc, sent[0])

@@ -4,13 +4,13 @@ from concourse.mybir import AluOpType as A, ActivationFunctionType as F
 ETA, DEL = 2.0 ** -24, 2.0 ** -12
 N, ND, NR, RO = 8, 2048, 4096, 2
 DT = {"F": "float32", "B": "bfloat16", "H": "float16", "I": "int32", "U": "uint16"}
-BIG = ("ACT I 2048;REG B 4352;PAYT B 2048;BT F 2048;T5 I 2048;T12 I 2048;n0i I 16;XR B 256;VI I 512;LC B 2048;SelN H 2048;LP B 2048;LT H 2048;P B 4096;"
-       "MN B 4096;E H 4096;W0 B 4096;W1 B 4096;LAND0 B 512;LAND1 B 512;NZ0 B 256;NZ1 B 256;ZL0 B 256;ZL1 B 256")
-SMALL = ("VI15 I 512;HPv B 512;HP15 B 512;KBr B 128;KBa B 128;KB B 128;pI I 8;pA I 8;pc F 16;JI F 16;JU U 16;I16 F 16;LTC F 16;LM F 256;DIAGN F 256;BO B 128;"
-         "BOx B 128;BOw B 128;BOn H 128;BOf H 128;EM H 128;SelNb B 256;D H 128;D2 H 128;t1 F 128;t2 F 128;t3 F 128;t4 F 128;t5 F 128;t6 F 128;m8 F 128;d2a F 128;d2b F 128;"
-         "d2c F 128;IDh H 128;IDb B 128;SHb B 128;RV B 384;RW B 384;CWa F 128;CWb F 128;CW B 128;ZMa F 128;ZM B 128;ONES B 128;ZF F 128;ZB B 256;TRASH F 16;ADDK H 8;"
+BIG = ("ACT I 2048;REG B 4352;PAYT B 2048;BT F 2048;T5 I 2048;T12 I 2048;n0i I 16;XR B 256;VI I 512;LC B 2048;LP B 2048;LT B 2048;SelN H 2048;P B 4096;"
+       "MN B 4096;E B 4096;W B 4096;LAND0 B 512;LAND1 B 512;NZ0 B 256;NZ1 B 256;ZL0 B 256;ZL1 B 256")
+SMALL = ("VI15 I 512;HPv B 512;HP15 B 512;KBr B 128;KBa B 128;KB B 128;pI I 8;pA I 8;pc F 16;JI F 16;JU U 16;I16 F 16;LM F 256;MSK F 256;BO B 128;"
+         "BOx B 128;BOw B 128;BOn H 128;EM H 128;SelNb B 256;D H 128;D2 H 128;t1 F 128;t2 F 128;t3 F 128;t4 F 128;t5 F 128;t6 F 128;m8 F 128;d2a F 128;d2b F 128;"
+         "d2c F 128;IDh H 128;ID13 H 128;IDb B 128;SHb B 128;RV B 384;RW B 384;CWa F 128;CWb F 128;CW B 128;ZMa F 128;ZM B 128;ONES B 128;ZF F 128;ZB B 256;TRASH F 16;ADDK H 48;"
          "NU0 U 16;A1 U 256;G5 I 256;G12 I 256;Bg1 F 256;bhI I 256;blI I 256;bh B 256;bl B 256;nA I 16;nB I 16;nC I 16;nD I 16;Nh F 16;Nl F 16;NMXh B 256;NMXl B 256;"
-         "A16 U 256;Bg F 256;V1 F 512;CM H 256;Tt F 256;Q H 512;Pk B 256;ADDL H 32;LI I 32;L2 I 32;LU U 128;NI I 16;NN I 16;Na I 16;Nb I 16;LIVE F 16;CNT F 256;QC H 256;"
+         "A16 U 256;Bg F 256;V1 F 512;CM H 256;Tt F 256;Q H 512;Pk B 256;NF H 16;LI I 32;L2 I 32;LU U 128;NI I 16;NN I 16;LIVE F 16;CNT F 256;"
          "SL U 32;KU U 16;OFF I 16;ph B 256;pl B 256;SC B 512;oa I 16;ob I 16;oc I 16;od I 16;oe I 16;ZIX U 16;GO F 16;KI I 16;KJ I 16;AI I 32;AU U 32;KBs H 256;dead F 16;"
          "KM F 16;KL F 16;DPs H 256;w1 F 16;w2 F 16;w3 F 16;w4 F 16;w5 F 16;OW U 32;XS B 256;VAL B 256;NEW B 256;NEWc B 256;OLD B 256")
 SCRATCH, WHERE, _fill = {}, {}, {}
@@ -27,7 +27,7 @@ for _d in _fill:
 for _i in range(8):
     SCRATCH["ps%d" % _i] = ("psum", [128, 512], "float32")
     WHERE["ps%d" % _i] = ("ps%d" % _i, 0, 512)
-SEMAPHORES = ["qV", "qS", "qT", "qG", "loc", "ldn0", "ldacts", "ldregs", "ldpay", "ldrch", "lddr", "st"]
+SEMAPHORES = ["qV", "qS", "qT", "qG", "locH", "locZ", "ldn0", "ldacts", "ldregs", "ldpay", "ldrch", "lddr", "st"]
 for _t in range(RO):
     SEMAPHORES += ["hA%d" % _t, "hB%d" % _t, "zA%d" % _t, "zB%d" % _t]
 
@@ -161,7 +161,6 @@ def rank_program(g, core, T, topo):
     dma("Y", T.n0i[:, :], T.n0[:, :], "ldn0", [], [v("n0i")])
     dma("Y", T.ACT[:, :], T.acts[:, :], "ldacts", [], [v("ACT")])
     dma("Y", T.REG[:, 0:NR], T.regs[:, :], "ldregs", [], [v("REG", 0, NR)])
-    dma("Y", T.PAYT[:, :], T.pay[:, :], "ldpay", [], [v("PAYT")])
     dma("S", T.XR[:, :], T.rch[:, :], "ldrch", [], [v("XR")])
     fill(v("VI"), 0)
     need("S", [("qV", cnt["V"], {})])
@@ -169,7 +168,10 @@ def rank_program(g, core, T, topo):
         for e, row in ((1, 6), (2, 2), (3, 4)):
             c = (t * 3 + e - 1) * 256
             g.scalar.dma_start(T.VI[row::16, t * 256:t * 256 + 256], T.dr[:, c:c + 256]).then_inc(T.sem["lddr"], 16)
-    note("lddr", [], [v("VI")], ("lddr", 96, dict(clk["S"])))
+    ldr = ("lddr", 96, dict(clk["S"]))
+    note("lddr", [], [v("VI")], ldr)
+    need("Y", [ldr])
+    dma("Y", T.PAYT[:, :], T.pay[:, :], "ldpay", [], [v("PAYT")])
 
     def iota(name, pattern, cm, **kw):
         op("G", lambda: g.iota(ap(v(name)), pattern, 0, cm, **kw), [], [v(name)])
@@ -187,32 +189,34 @@ def rank_program(g, core, T, topo):
     fill(v("ZF"), 0.0)
     fill(v("ZB"), 0.0)
     for d in range(N):
-        fill(v("W0", 512 * d, 512 * d + 64), 0.0)
+        fill(v("W", 512 * d, 512 * d + 64), 0.0)
     ts(v("pA"), v("pI"), 15, A.bitwise_and)
-    pc = [v("pc", i, i + 1) for i in range(9)]
+    pc = [v("pc", i, i + 1) for i in range(12)]
     cp(pc[0], v("pA", 0, 1))
     cp(v("JU"), v("JI"))
-    for i, m, a in ((1, 1, 1), (2, 1, -7), (3, 1, -8), (4, -256, 1), (5, 16, -2032), (6, 1, 4096)):
+    for i, m, a in ((1, 1, 1), (2, 1, -7), (3, 1, -8), (4, -256, 1), (5, 16, -2032), (9, 16, -2034), (10, 16, -2035), (6, 1, 4096)):
         ts(pc[i], pc[0], float(m), A.mult, float(a), A.add)
     KB, JI = v("KB"), v("JI")
     ts(v("I16"), JI, pc[0], A.is_equal)
-    ts(v("LTC"), JI, pc[0], A.is_gt)
     ts(v("BO"), KB, 0.0, A.is_ge)
     ts(v("t6"), KB, 15.0, A.is_equal)
     ts(pc[7], v("I16", 0, 1), 64.0, A.mult, v("I16", 1, 2), A.add)
     tt(pc[8], v("I16", 7, 8), v("I16", 15, 16), A.add)
+    ts(pc[11], v("I16", 0, 1), 64.0, A.mult)
     tt(v("BOx"), v("BO"), v("t6"), A.subtract)
     ts(v("BOw"), v("BO"), pc[7], A.mult)
     for k in range(16):
         aff(B("LC", k), v("BOx") if k < 8 else v("BO"), [[0, 8], [1, 16]], A.is_ge, 0.0, -k, 0)
     for j in range(16):
         aff(B("LP", j), v("BOw"), [[0, 8], [1, 16]], A.is_equal, 0.0, -j, 0)
+    for j in range(1, 16):
+        aff(B("LT", j), v("BO"), [[16, 8], [0, 16]], A.is_ge, 0.0, j - 1, -1)
     ts(v("EM"), v("BO"), pc[8], A.mult)
-    ts(v("DIAGN"), v("LM"), pc[0], A.is_equal, -1.0, A.mult)
+    ts(v("MSK"), v("LM"), pc[0], A.is_equal, -1.0, A.mult)
     ts(v("TRASH"), JI, 16.0, A.mult, pc[6], A.add)
-    ts(v("ADDK"), v("JI", 0, 8), 256.0, A.mult, pc[5], A.add)
+    for lev, i in ((1, 5), (2, 9), (3, 10)):
+        ts(B("ADDK", lev - 1, 16), JI, 256.0, A.mult, pc[i], A.add)
     ts(v("BOn"), KB, 0.0, A.is_ge, -1.0, A.mult)
-    ts(v("BOf"), KB, 0.0, A.is_ge)
     for i, r in enumerate((6, 2, 4)):
         ts(B("RV", i), v("BO"), v("I16", r, r + 1), A.mult)
     for i, r in enumerate((6, 3, 5)):
@@ -233,19 +237,19 @@ def rank_program(g, core, T, topo):
     tt(v("d2c"), v("d2a"), v("d2b"), A.add)
     cp(v("NU0"), v("n0i"))
     cp(v("IDh"), v("t2"))
+    ts(v("ID13"), v("t2"), 13.0, A.mult)
     tt(v("D2"), v("d2c"), v("m8"), A.mult)
     cp(v("IDb"), v("t2"))
     cp(v("SHb"), v("t1"))
-    for j in range(16):
-        ts(B("SelN", j), KB, float(j), A.is_equal, -1.0, A.mult)
     for j in range(2):
         ts(B("SelNb", j), KB, float(j), A.is_equal, -1.0, A.mult)
+    ts(v("nA"), v("n0i"), 13.0, A.mult, 1.0, A.add)
     for h in range(2):
         cpg(B("A1", h), v("ACT"), B("NU0", h, 8))
-    ts(v("nA"), v("n0i"), 13.0, A.mult, 1.0, A.add)
-    ts(v("G5"), v("A1"), 5.0, A.mult)
+    for j in range(16):
+        ts(B("SelN", j), KB, float(j), A.is_equal, -1.0, A.mult)
     ts(v("nB"), v("nA"), ND - 1, A.bitwise_and)
-    ts(v("G12"), v("G5"), 4095, A.bitwise_and)
+    ts(v("G5"), v("A1"), 5.0, A.mult)
     ts(v("nC"), v("nB"), 6, A.logical_shift_right)
     ts(v("nD"), v("nB"), 63, A.bitwise_and)
     ts(v("bhI"), v("G5"), 6, A.logical_shift_right, 31, A.bitwise_and)
@@ -253,71 +257,74 @@ def rank_program(g, core, T, topo):
     cp(v("Nl"), v("nD"))
     ts(v("blI"), v("G5"), 63, A.bitwise_and)
     cp(v("bh"), v("bhI"))
-    ttg(v("NMXh"), v("Nh"), v("JU"), v("DIAGN"), A.mult)
-    ttg(v("NMXl"), v("Nl"), v("JU"), v("DIAGN"), A.mult)
+    ttg(v("NMXh"), v("Nh"), v("JU"), v("MSK"), A.mult)
+    ttg(v("NMXl"), v("Nl"), v("JU"), v("MSK"), A.mult)
     cp(v("bl"), v("blI"))
     cp(v("ps0", 256, 512), v("XR"))
-    ts(v("VI15"), v("VI"), 15, A.bitwise_and)
-    cp(v("HPv"), v("VI"))
-    cp(v("HP15"), v("VI15"))
     ts(v("T5"), v("ACT"), 5.0, A.mult)
-    ts(v("T12"), v("T5"), 4095, A.bitwise_and)
+    ts(v("VI15"), v("VI"), 15, A.bitwise_and)
+    cp(v("HPv", 0, 256), v("VI", 0, 256))
+    ts(v("HPv", 256, 512), v("VI", 256, 512), pc[11], A.add)
+    cp(v("HP15"), v("VI15"))
 
-    def later_constants():
-        ts(v("BT"), v("T12"), -2048.0, A.add)
-        ts(v("ZMa"), v("t2"), 16.0, A.mult)
-        for h in range(2):
-            cp(B("ADDL", 2 * h + 1, 8), v("ADDK"))
-        tt(v("ZM"), v("ZMa"), v("BO"), A.subtract)
-        for d in range(N):
-            fill(v("W1", 512 * d, 512 * d + 64), 0.0)
+    def Cb(p):
+        return v("ps%d" % (1 + p), 0, 128)
 
-    def Cb(h):
-        return v("ps%d" % (1 + h), 0, 128)
-
-    def Mb(h, a=0, b=128):
-        return v("ps%d" % (3 + h), a, b)
+    def Mb(p, a, b):
+        return v("ps%d" % (3 + p), a, b)
 
     recs = v("REG", 0, NR)
+    todo = []
 
-    def minima(h, xcol, lev, draws15, ks=range(16)):
-        for k in ks:
-            mk = B("MN", 16 * h + k)
-            tt(mk, v("P", 2048 * h + k, 2048 * h + 2048, 16), v("ps0", xcol + 128 * h, xcol + 128 * h + 128), A.min)
+    def gap(n):
+        while n > 0 and todo:
+            todo.pop(0)()
+            n -= 1
+
+    def minima(p, x, lev, draws15):
+        def one(k):
+            mk = B("MN", 16 * p + k)
+            tt(mk, v("P", 2048 * p + k, 2048 * p + 2048, 16), x, A.min)
             if k == 0:
-                mm(Mb(h), v("CW"), v("ONES"), True, False)
-                mm(Mb(h), B("RW", lev - 1), draws15, False, False)
-            mm(Cb(h), B("LC", k), mk, k == 0, k == 15)
+                mm(Mb(p, 0, 128), v("CW"), v("ONES"), True, False)
+                mm(Mb(p, 0, 128), B("RW", lev - 1), draws15, False, False)
+            mm(Cb(p), B("LC", k), mk, k == 0, k == 15)
+        return [lambda k=k: one(k) for k in range(16)]
 
-    def decide(h, v1, gap=lambda: None):
-        cp(B("CM", h), Cb(h))
-        mm(Mb(h), v("EM"), B("CM", h), False, True)
-        gap()
-        tt(B("Tt", h), Mb(h), v1, A.mult)
-        tt(cond(h), Cb(h), B("Tt", h), A.is_gt)
+    def cond(p):
+        return B("Q", 2 * p + 1)
 
-    def cond(h, j=None):
-        return B("Q", 2 * h + 1) if j is None else v("Q", 256 * h + 128 + j, 256 * h + 256, 16)
+    def decide(p, v1, n):
+        cp(B("CM", p), Cb(p))
+        mm(Mb(p, 0, 128), v("EM"), B("CM", p), False, True)
+        gap(n)
+        tt(B("Tt", p), Mb(p, 0, 128), v1, A.mult)
+        gap(n)
+        tt(cond(p), Cb(p), B("Tt", p), A.is_gt)
 
-    def chosen(h, lists):
-        act(B("Pk", h), B("P", h, 2048), F.Identity, off=lists, bias=1.0)
+    def listed(out, name, a, b, more=False):
+        for j in range(16):
+            mm(out, B("SelN", j), v(name, a + j, b, 16), j == 0, j == 15 and not more)
+
+    def chosen(p, lists):
+        act(B("Pk", p), B("P", p, 2048), F.Identity, off=lists, bias=1.0)
 
     def thresholds(out, ps):
         act(out, ps, F.Identity, scale=1.0 / 64, bias=DEL / 64)
 
-    sent = [0]
+    sent = {"locH": 0, "locZ": 0}
     plans = [plan(r, cores, topo) for r in range(N)]
     mine = q // 4
     order = (mine, 1 - mine)
 
-    def send(src, dst, width, swidth, call, sem):
+    def send(src, dst, width, swidth, call, sem, loc):
         tr = []
         for r, e in plans[q][call]:
             rid, pid, _ = topo.addr(cores[r])
             tr.append(RemoteDMATransfer(dst_ids=[DstId(rid=rid, pnc=pid)], dma_engine_mask=sum(1 << x for x in e), remote_sem=T.sem[sem],
                                         srcs=[T[src][:, r * swidth:r * swidth + width]], dsts=[T[dst][:, q * width:q * width + width]]))
-            sent[0] += len(e)
-        g.remote_dma_fused(tr, local_sem=T.sem.loc)
+            sent[loc] += len(e)
+        g.remote_dma_fused(tr, local_sem=T.sem[loc])
 
     def landed(buf, width, sems):
         for i, h in enumerate(order):
@@ -326,38 +333,33 @@ def rank_program(g, core, T, topo):
                 if r != q:
                     note(sems[i], [], [B(buf, r, width)], (sems[i], val, {}))
 
-    def sel(j):
-        return B("SelN", j)
+    def key_sums(p):
+        mm(B("ps7", 1 + p), v("BOn"), B("Q", 2 * p), True, True)
+        listed(B("ps7", p, 8), "Q", 256 * p, 256 * p + 128)
 
     def keys(h, live):
         kl, KMh, KLh, dd = B("ps7", h, 8), B("KM", h, 8), B("KL", h, 8), B("dead", h, 8)
-        lv = (live[0], live[1] + 8 * h, live[1] + 8 * h + 8, 1)
-        mm(B("ps7", 1 + h), v("BOn"), B("Q", 2 * h), True, True)
-        for j in range(16):
-            mm(kl, sel(j), v("Q", 256 * h + j, 256 * h + 128, 16), j == 0, j == 15)
-        ts(dd, lv, -9999.0, A.mult, 9999.0, A.add)
-        cp(B("KBs", h), B("ps7", 1 + h))
-        tt(KMh, kl, lv, A.mult)
-        ts(B("KI", h, 8), kl, 2048.0, A.add)
-        tt(KLh, KMh, dd, A.add)
+        lv = B(live, h, 8)
+        return [lambda: ts(dd, lv, -9999.0, A.mult, 9999.0, A.add), lambda: cp(B("KBs", h), B("ps7", 1 + h)), lambda: tt(KMh, kl, lv, A.mult),
+                lambda: ts(B("KI", h, 8), kl, 2048.0, A.add), lambda: tt(KLh, KMh, dd, A.add)]
 
     def matches(c, a, b):
         e = lambda x: 240 * c + x
         ts(v("E", e(a), e(b)), v("KBs", a, b), v("KL", c, c + 1), A.is_equal)
         a = max(a, 16 * c + 16)
         if a < b:
-            mm(v("ps6", 256 + a, 256 + b), v("BOf"), v("E", e(a), e(b)), False, False)
+            mm(v("ps6", 256 + a, 256 + b), v("BO"), v("E", e(a), e(b)), False, False)
 
-    def inner(h, cs):
-        for c in cs:
-            matches(8 * h + c, 16 * (8 * h + c), 128 * h + 128)
+    def inner(h):
+        return [lambda c=c: matches(c, 16 * c, 128 * h + 128) for c in range(8 * h, 8 * h + 8)]
+
+    def across():
+        return [lambda c=c: matches(c, 128, 256) for c in range(8)]
 
     def open_sums():
         mm(v("ps6", 256, 512), v("BO"), v("ZB"), True, False)
 
     def finish_sums(i, live):
-        for c in range(8):
-            matches(c, 128, 256)
         for j in range(1, 16):
             mm(v("ps6", 256 + j, 512, 16), B("LT", j), v("E", j, 4096, 256), False, j == 15)
         ai = B("AI", i, 16)
@@ -365,16 +367,14 @@ def rank_program(g, core, T, topo):
         ts(ai, v("KJ"), NR - 1, A.bitwise_and)
         cp(B("AU", i, 16), ai)
         tt(v("w3"), ai, v("TRASH"), A.subtract)
-        tt(v("w4"), v("w3"), live, A.mult)
+        tt(v("w4"), v("w3"), v(live), A.mult)
 
     def winners(i):
-        cp(v("DPs"), v("ps6", 256, 512))
-        for j in range(16):
-            mm(v("ps7", 32, 48), sel(j), v("DPs", j, 256, 16), j == 0, j == 15)
-        ts(v("w1"), v("ps7", 32, 48), 0.0, A.is_equal)
-        tt(v("w2"), v("w1"), v("w4"), A.mult)
-        tt(v("w5"), v("w2"), v("TRASH"), A.add)
-        cp(B("OW", i, 16), v("w5"))
+        def one():
+            cp(v("DPs"), v("ps6", 256, 512))
+            listed(v("ps7", 32, 48), "DPs", 0, 256)
+        return [one, lambda: ts(v("w1"), v("ps7", 32, 48), 0.0, A.is_equal), lambda: tt(v("w2"), v("w1"), v("w4"), A.mult),
+                lambda: tt(v("w5"), v("w2"), v("TRASH"), A.add), lambda: cp(B("OW", i, 16), v("w5"))]
 
     def change(win, off, other, o, i):
         ttg(v("NEW"), win, off, other, o)
@@ -382,161 +382,181 @@ def rank_program(g, core, T, topo):
         scat(v("REG"), B("OW", i, 16), v("NEWc"))
 
     for t in range(RO):
-        W, LAND, NZ, ZL = "W%d" % t, "LAND%d" % t, "NZ%d" % t, "ZL%d" % t
-        for h in range(2):
-            act(B("P", h, 2048), recs, F.Relu, off=B("A1", h))
-            if h == 0:
-                mm(v("ps5", 0, 256), B("RV", 0), B("HPv", t, 256), True, True)
-                thresholds(v("V1", 0, 256), v("ps5", 0, 256))
+        LAND, NZ, ZL = "LAND%d" % t, "NZ%d" % t, "ZL%d" % t
 
-        def pay(h):
-            o = B("ps5", 2 + h)
-            mm(o, v("IDb"), B("HPv", 2 * t + h), True, False)
-            mm(o, v("SHb"), B("HP15", 2 * t + h), False, False)
+        def places(p):
+            decide(p, B("V1", p), 1)
+            oh, ohd, lst = Mb(p, 128, 256), Mb(p, 256, 384), Mb(p, 384, 400)
+            mm(ohd, v("D2"), cond(p), True, True)
+            mm(oh, v("D"), cond(p), True, True)
+            gap(2)
+            init = pc[4] if p == 0 else v("CNT", 127, 128)
+            op("V", lambda: g.vector.tensor_tensor_scan(ap(B("CNT", p)), ap(ohd), ap(v("ZF")), ap(init), A.add, A.add), [ohd, v("ZF"), init], [B("CNT", p)])
+            tt(B("ph", p), oh, B("bh", p), A.mult)
+            tt(B("Q", 2 * p), ohd, B("CNT", p), A.mult)
+            tt(B("pl", p), oh, B("bl", p), A.mult)
+            listed(lst, "Q", 256 * p, 256 * p + 256, True)
+            mm(Mb(p, 392, 400), v("IDh"), v("ADDK", 0, 8), False, True)
+            o = B("ps5", 2 + p)
+            mm(o, v("IDb"), B("HPv", 2 * t + p), True, False)
+            mm(o, v("SHb"), B("HP15", 2 * t + p), False, False)
             for name, i in (("NMXh", 0), ("NMXl", 1), ("ph", 0), ("pl", 1)):
-                mm(o, B("SelNb", i), B(name, h), False, name == "pl")
-            act(B("SC", 2 * h + 1), o, F.Copy)
+                mm(o, B("SelNb", i), B(name, p), False, name == "pl")
+            gap(6)
+            ts(B("KU", p, 8), Mb(p, 392, 400), 2048.0, A.add)
+            ts(B("SL", 2 * p + 1, 8), Mb(p, 384, 392), -2.0, A.mult, 1.0, A.add)
+            ts(B("SL", 2 * p, 8), Mb(p, 384, 392), -2.0, A.mult)
+            chosen(p, B("KU", p, 8))
+            act(B("SC", 2 * p + 1), o, F.Copy)
 
-        def places(h):
-            mm(Mb(h, 256, 384), v("D2"), cond(h), True, True)
-            mm(Mb(h, 128, 256), v("D"), cond(h), True, True)
-            init = pc[4] if h == 0 else v("CNT", 127, 128)
-            op("V", lambda: g.vector.tensor_tensor_scan(ap(B("CNT", h)), ap(Mb(h, 256, 384)), ap(v("ZF")), ap(init), A.add, A.add),
-               [Mb(h, 256, 384), v("ZF"), init], [B("CNT", h)])
-            tt(B("ph", h), Mb(h, 128, 256), B("bh", h), A.mult)
-            tt(B("QC", h), Mb(h, 256, 384), B("CNT", h), A.mult)
-            tt(B("pl", h), Mb(h, 128, 256), B("bl", h), A.mult)
-            for j in range(16):
-                mm(Mb(h, 400, 408), sel(j), v("QC", 128 * h + j, 128 * h + 128, 16), j == 0, j == 15)
-            mm(Mb(h, 384, 392), v("IDh"), v("ADDK"), True, False)
-            for j in range(16):
-                mm(Mb(h, 384, 392), sel(j), cond(h, j), False, j == 15)
+        def xpay(p):
+            tt(B("SC", 2 * p), B("ps0", 2 + p), B("Pk", p), A.min)
 
-        def lists(h):
-            ts(B("KU", h, 8), Mb(h, 384, 392), 2048.0, A.add)
-            ts(B("SL", 2 * h + 1, 8), Mb(h, 400, 408), -2.0, A.mult, 1.0, A.add)
-            ts(B("SL", 2 * h, 8), Mb(h, 400, 408), -2.0, A.mult)
-            chosen(h, B("KU", h, 8))
-
-        def xpay(h):
-            tt(B("SC", 2 * h), B("ps0", 2 + h), B("Pk", h), A.min)
-
-        minima(0, 256, 1, B("HP15", 2 * t))
-        decide(0, B("V1", 0))
+        act(v("P", 0, 1024), recs, F.Relu, off=v("A1", 0, 64))
+        op("V", lambda: g.vector.tensor_scalar(ap(v("P", 1024, 2048)), ap(recs).indirect(ap(v("A1", 64, 128))), 0.0, None, A.max),
+           [recs, v("A1", 64, 128)], [v("P", 1024, 2048)])
+        act(B("P", 1, 2048), recs, F.Relu, off=B("A1", 1))
+        mm(v("ps5", 0, 256), B("RV", 0), B("HPv", t, 256), True, True)
+        thresholds(v("V1", 0, 256), v("ps5", 0, 256))
+        todo += minima(0, B("ps0", 2), 1, B("HP15", 2 * t))
+        gap(16)
+        if t:
+            need("V", [("locH", sent["locH"], {})])
+        todo += minima(1, B("ps0", 3), 1, B("HP15", 2 * t + 1))
         places(0)
-        pay(0)
-        minima(1, 256, 1, B("HP15", 2 * t + 1), range(8))
-        lists(0)
-        minima(1, 256, 1, B("HP15", 2 * t + 1), range(8, 16))
-        decide(1, B("V1", 1), lambda: xpay(0))
+        gap(99)
+        todo += [lambda: xpay(0), lambda: scat(v("W"), B("SL", 0, 16), B("SC", 0, 256))]
         places(1)
-        pay(1)
-        scat(v(W), B("SL", 0, 16), B("SC", 0, 256))
-        lists(1)
-        scat(v(W), B("SL", 3, 8), B("SC", 3))
+        gap(99)
+        scat(v("W"), B("SL", 3, 8), B("SC", 3))
         xpay(1)
-        scat(v(W), B("SL", 2, 8), B("SC", 2))
-        need("G", deps("G", [v(W)], []))
+        scat(v("W"), B("SL", 2, 8), B("SC", 2))
+        need("G", deps("G", [v("W")], []))
         for i in range(2):
-            send(W, LAND, 64, 512, i, "h%s%d" % ("AB"[i], t))
-        for h in range(2):
-            tt(B("Q", 2 * h), Mb(h, 128, 256), B("Bg1", h), A.mult) if t else None
+            send("W", LAND, 64, 512, i, "h%s%d" % ("AB"[i], t), "locH")
         if t == 0:
+            ts(v("G12"), v("G5"), 4095, A.bitwise_and)
             ts(v("Bg1"), v("G12"), -2048.0, A.add)
-            for h in range(2):
-                tt(B("Q", 2 * h), Mb(h, 128, 256), B("Bg1", h), A.mult)
-        cp(B(LAND, q, 64), v(W, 512 * q, 512 * q + 64))
-        for h in range(2):
-            ts(B("OFF", h, 8), Mb(h, 400, 408), -1.0, A.mult)
+        for p in range(2):
+            tt(B("Q", 2 * p), Mb(p, 128, 256), B("Bg1", p), A.mult)
+            key_sums(p)
+        cp(B(LAND, q, 64), v("W", 512 * q, 512 * q + 64))
+        for p in range(2):
+            ts(B("OFF", p, 8), Mb(p, 384, 392), -1.0, A.mult)
+        open_sums()
         ts(v("oc"), v("OFF"), 255, A.bitwise_and)
         ts(v("oa"), v("OFF"), 8, A.logical_shift_right)
-        ts(v("ob"), v("OFF"), 31, A.bitwise_and)
         ts(v("GO"), v("oc"), 32.0, A.is_lt)
+        ts(v("ob"), v("OFF"), 31, A.bitwise_and)
         ts(v("od"), v("oa"), 32.0, A.mult)
-        if t == 0:
-            for j in range(1, 16):
-                ts(B("LT", j), v("BO"), v("LTC", j, j + 1), A.mult)
-            later_constants()
+        todo += [f for two in zip(keys(0, "GO"), keys(1, "GO")) for f in two] + [lambda c=c: matches(c, 16 * c, 256) for c in range(16)]
+        gap(99)
         tt(v("oe"), v("od"), v("ob"), A.add)
-        open_sums()
-        keys(0, v("GO"))
-        keys(1, v("GO"))
+        finish_sums(0, "GO")
         cp(v("ZIX"), v("oe"))
-        for h in range(2):
-            inner(h, range(8))
-        finish_sums(0, v("GO"))
+        if t == 0:
+            ts(v("T12"), v("T5"), 4095, A.bitwise_and)
+            ts(v("ZMa"), v("t2"), 16.0, A.mult)
 
         landed(LAND, 64, ("hA%d" % t, "hB%d" % t))
 
-        def gathers(h, off):
-            cpg(B("A16", h), v("ACT"), off)
-            return lambda: (act(B("P", h, 2048), recs, F.Relu, off=B("A16", h)), act(B("Bg", h), v("BT"), F.Copy, off=off))
+        def gathers(p, off):
+            cpg(B("A16", p), v("ACT"), off)
+            act(B("P", p, 2048), recs, F.Relu, off=B("A16", p))
 
-        def nextn(h, node, lev):
-            ts(B("Na", h, 8), node, 13.0, A.mult, float(lev), A.add)
-            ts(B("Nb", h, 8), B("Na", h, 8), ND - 1, A.bitwise_and)
-            cp(B("ADDL", 2 * h, 8), B("Nb", h, 8))
+        def more(p, off):
+            act(B("Bg", p), v("BT"), F.Copy, off=off)
 
-        def receive(h):
-            o, odd = Mb(h, 384, 392), v(LAND, 256 * h + 1, 256 * h + 256, 2)
+        def receive(h, ps):
+            o = v("ps7", 48 + 8 * h, 56 + 8 * h)
             for j in range(16):
                 mm(o, B("LP", j), v(LAND, 256 * h + 2 * j + 1, 256 * h + 256, 32), j == 0, j == 15)
-            ni, nn = B("NI", h, 8), B("NN", h, 8)
+            ni, nn, lu = B("NI", h, 8), B("NN", h, 8), B("LU", h, 8)
             cp(ni, o)
             ts(nn, ni, ND - 1, A.bitwise_and)
-            cp(B("LU", 8 * h, 8), nn)
-            gathers(h, B("LU", 8 * h, 8))()
+            cp(lu, nn)
+            cpg(B("A16", h), v("ACT"), lu)
             for i in (0, 1):
-                mm(B("ps5", 2 * h + i), B("RV", 1 + i), odd, True, True)
-            thresholds(B("V1", h, 256), B("ps5", h, 256))
+                mm(B(ps, i), B("RV", 1 + i), v(LAND, 256 * h + 1, 256 * h + 256, 2), True, True)
+            act(B("P", h, 2048), recs, F.Relu, off=B("A16", h))
+            thresholds(B("V1", h, 256), v(ps, 0, 256))
             cp(B("ps0", h), v(LAND, 256 * h, 256 * h + 256, 2))
-            nextn(h, nn, 2)
-            ts(B("LIVE", h, 8), ni, 4096.0, A.is_ge)
+            cp(B("NF", h, 8), nn)
+            ts(B("LIVE", h, 8), ni, 4096.0 * (t + 1), A.is_ge)
 
-        def far(h, lev, gaps=()):
-            gaps = list(gaps) + [lambda: None] * 9
-            minima(h, 0, lev, v(LAND, 256 * h + 1, 256 * h + 256, 2))
-            decide(h, B("V1", 2 * h + lev - 2), gaps[0])
-            mm(Mb(h, 128, 256), v("D"), cond(h), True, True)
-            gaps[1]()
-            tt(B("Q", 2 * h), Mb(h, 128, 256), B("Bg", h), A.mult)
-            o = Mb(h, 384, 400)
-            mm(o, v("IDh"), B("ADDL", h, 16), True, False)
-            for j in range(16):
-                mm(o, sel(j), v("Q", 256 * h + j, 256 * h + 256, 16), False, j == 15)
-            gaps[2]()
-            ts(B("LI", h, 16), o, 2048.0, A.add)
-            ts(B("L2", h, 16), B("LI", h, 16), ND - 1, A.bitwise_and)
-            b = 64 * h + 16 * (lev - 1)
-            cp(v("LU", b, b + 16), B("L2", h, 16))
-            x, node = B("ps0", h), v("LU", b, b + 8)
-            later = gathers(h, node) if lev == 2 else None
-            chosen(h, v("LU", b + 8, b + 16))
+        def minima23(p, lev):
+            return minima(p, B("ps0", p), lev, v(LAND, 256 * p + 1, 256 * p + 256, 2))
+
+        def far(p, lev, n):
+            decide(p, B("V1", 2 * p + lev - 2), n[0])
+            mm(Mb(p, 128, 256), v("D"), cond(p), True, True)
+            gap(n[1])
+            tt(B("Q", 2 * p), Mb(p, 128, 256), B("Bg", p), A.mult)
+            listed(Mb(p, 384, 400), "Q", 256 * p, 256 * p + 256, True)
+            mm(Mb(p, 384, 392), v("ID13"), B("NF", p, 8), False, False)
+            mm(Mb(p, 392, 400), v("IDh"), v("ADDK", 16 * lev - 16, 16 * lev - 8), False, True)
+            if lev == 3:
+                key_sums(p)
+            gap(n[2])
+            ts(B("LI", p, 16), Mb(p, 384, 400), 2048.0 + lev, A.add)
+            gap(n[3])
+            ts(B("L2", p, 16), B("LI", p, 16), ND - 1, A.bitwise_and)
+            gap(n[3])
+            b = 16 + 32 * (lev - 2) + 16 * p
+            cp(v("LU", b, b + 16), B("L2", p, 16))
             if lev == 2:
-                later()
-                nextn(h, B("L2", 2 * h, 8), 3)
-                tt(x, x, B("Pk", h), A.min)
-            else:
-                gaps[3]()
-                tt(B("XS", h), x, B("Pk", h), A.min)
-                ttg(B("VAL", h), v("PAYT"), node, B("XS", h), A.min)
-                mm(Cb(h), v("ZM"), B("VAL", h), True, True)
-                act(B(NZ, h), Cb(h), F.Sign, scale=-1.0)
-                need("G", deps("G", [B(NZ, h)], []))
-                send(NZ, ZL, 32, 32, int(h != mine), "z%s%d" % ("AB"[int(h != mine)], t))
+                cpg(B("A16", p), v("ACT"), v("LU", b, b + 8))
+            chosen(p, v("LU", b + 8, b + 16))
+            if lev == 2:
+                act(B("P", p, 2048), recs, F.Relu, off=B("A16", p))
+                more(p, v("LU", b, b + 8))
+                cp(B("NF", p, 8), B("L2", 2 * p, 8))
+                gap(n[4])
+                tt(B("ps0", p), B("ps0", p), B("Pk", p), A.min)
+
+        def leaf(p):
+            tt(B("XS", p), B("ps0", p), B("Pk", p), A.min)
+            ttg(B("VAL", p), v("PAYT"), v("LU", 48 + 16 * p, 56 + 16 * p), B("XS", p), A.min)
+            mm(Cb(p), v("ZM"), B("VAL", p), True, True)
+            act(B(NZ, p), Cb(p), F.Sign, scale=-1.0)
+            i = int(p != mine)
+            need("G", deps("G", [B(NZ, p)], []))
+            send(NZ, ZL, 32, 32, i, "z%s%d" % ("AB"[i], t), "locZ")
 
         a, b = order
-        receive(a)
-        winners(0)
-        receive(b)
-        far(a, 2)
-        far(b, 2)
-        far(a, 3)
-        far(b, 3, (lambda: (open_sums(), keys(a, v("LIVE"))), lambda: inner(a, range(2)), lambda: inner(a, range(2, 8)), lambda: keys(b, v("LIVE"))))
-        inner(b, range(8))
-        finish_sums(1, v("LIVE"))
+        receive(a, "ps5")
+        todo += winners(0)
+        gap(2)
+        receive(b, "ps6")
+        gap(99)
+        if t == 0:
+            ts(v("BT"), v("T12"), -2048.0, A.add)
+            tt(v("ZM"), v("ZMa"), v("BO"), A.subtract)
+        for p in order:
+            more(p, B("LU", p, 8))
+        todo += minima23(a, 2)
+        gap(16)
+        todo += minima23(b, 2)
+        far(a, 2, (0, 0, 5, 1, 2))
+        gap(99)
+        far(b, 2, (0, 0, 0, 0, 0))
+        todo += minima23(a, 3)
+        gap(16)
+        todo += minima23(b, 3)
+        far(a, 3, (0, 0, 5, 1, 0))
+        gap(99)
+        leaf(a)
+        todo += [open_sums] + keys(a, "LIVE") + inner(a)
+        far(b, 3, (2, 2, 6, 1, 0))
+        leaf(b)
+        gap(99)
+
+        todo += keys(b, "LIVE") + inner(b) + across()
+        gap(99)
+        finish_sums(1, "LIVE")
         cp(B(ZL, q, 32), B(NZ, q, 32))
-        winners(1)
+        todo += winners(1)
+        gap(99)
         change(recs, B("AU", 1, 16), v(NZ), A.subtract, 1)
         cpg(v("OLD"), recs, B("AU", 0, 16))
         landed(ZL, 32, ("zA%d" % t, "zB%d" % t))
@@ -546,4 +566,5 @@ def rank_program(g, core, T, topo):
     g.sync.wait_ge(T.sem.st, 16)
     for k in "VSTG":
         need("Y", [("q" + k, cnt[k], {})])
-    g.wait_ge(T.sem.loc, sent[0])
+    for k in sent:
+        g.wait_ge(T.sem[k], sent[k])

from concourse.bass import DstId, RemoteDMATransfer
from concourse.mybir import AluOpType as A, ActivationFunctionType as F

ETA, DEL = 2.0 ** -24, 2.0 ** -12
N, ND, NR, RO = 8, 2048, 4096, 2
DT = {"F": "float32", "B": "bfloat16", "H": "float16", "I": "int32", "U": "uint16"}
BIG = ("ACT I 2048;REG B 4352;PAYT B 2048;BT F 2048;T5 I 2048;T12 I 2048;n0i I 16;XR B 256;VI I 512;LC B 2048;LP B 2048;LT B 2048;SelN H 2048;P B 4096;"
       "MN B 4096;E B 4096;W B 4096;LAND0 B 512;LAND1 B 512;NZ0 B 256;NZ1 B 256;ZL0 B 256;ZL1 B 256")
SMALL = ("VI15 I 512;HPv B 512;HP15 B 512;KBr B 128;KBa B 128;KB B 128;pI I 8;pA I 8;pc F 16;JI F 16;JU U 16;I16 F 16;LM F 256;MSK F 256;BO B 128;"
         "BOx B 128;BOw B 128;BOn H 128;EM H 128;SelNb B 256;D H 128;D2 H 128;t1 F 128;t2 F 128;t3 F 128;t4 F 128;t5 F 128;t6 F 128;m8 F 128;d2a F 128;d2b F 128;"
         "d2c F 128;IDh H 128;ID13 H 128;IDb B 128;SHb B 128;RV B 384;RW B 384;CWa F 128;CWb F 128;CW B 128;ZMa F 128;ZM B 128;ONES B 128;ZF F 128;ZB B 256;TRASH F 16;ADDK H 48;"
         "NU0 U 16;A1 U 256;G5 I 256;G12 I 256;Bg1 F 256;bhI I 256;blI I 256;bh B 256;bl B 256;nA I 16;nB I 16;nC I 16;nD I 16;Nh F 16;Nl F 16;NMXh B 256;NMXl B 256;"
         "A16 U 256;Bg F 256;V1 F 512;CM H 256;Tt F 256;Q H 512;Pk B 256;NF H 16;LI I 32;L2 I 32;LU U 128;NI I 16;NN I 16;LIVE F 16;CNT F 256;"
         "SL U 32;KU U 16;OFF I 16;ph B 256;pl B 256;SC B 512;oa I 16;ob I 16;oc I 16;od I 16;oe I 16;ZIX U 16;GO F 16;KI I 16;KJ I 16;AI I 32;AU U 32;KBs H 256;dead F 16;"
         "KM F 16;KL F 16;DPs H 256;w1 F 16;w2 F 16;w3 F 16;w4 F 16;w5 F 16;OW U 32;XS B 256;VAL B 256;NEW B 256;NEWc B 256;OLD B 256")
SCRATCH, WHERE, _fill = {}, {}, {}
for _x in BIG.split(";"):
    _n, _d, _w = _x.split()
    SCRATCH[_n] = ("sbuf", [128, int(_w)], DT[_d])
    WHERE[_n] = (_n, 0, int(_w))
for _x in SMALL.split(";"):
    _n, _d, _w = _x.split()
    WHERE[_n] = ("pool" + _d, _fill.get(_d, 0), int(_w))
    _fill[_d] = _fill.get(_d, 0) + (int(_w) + 15) // 16 * 16
for _d in _fill:
    SCRATCH["pool" + _d] = ("sbuf", [128, _fill[_d]], DT[_d])
for _i in range(8):
    SCRATCH["ps%d" % _i] = ("psum", [128, 512], "float32")
    WHERE["ps%d" % _i] = ("ps%d" % _i, 0, 512)
SEMAPHORES = ["qV", "qS", "qT", "qG", "locH", "locZ", "ldn0", "ldacts", "ldregs", "ldpay", "ldrch", "lddr", "st"]
for _t in range(RO):
    SEMAPHORES += ["hA%d" % _t, "hB%d" % _t, "zA%d" % _t, "zB%d" % _t]


def plan(q, cores, topo):
    out = []
    mine = q // 4
    for half in (mine, 1 - mine):
        rs = [r for r in range(4 * half, 4 * half + 4) if r != q]
        far = [r for r in rs if topo.chip(cores[r]) != topo.chip(cores[q])]
        near = [r for r in rs if r not in far]
        call, used = [], []
        for grp in (far, near):
            for i, r in enumerate(grp):
                e = [x for x in topo.engines(cores[q], cores[r]) if grp is far or x not in used]
                n = len(e) // len(grp)
                call.append((r, e[i * n:(i + 1) * n]))
            used = [x for _, e in call for x in e]
        out.append(call)
    return out


def rank_program(g, core, T, topo):
    q = T.rank_of(core)
    if q is None:
        return
    cores = list(T.cores)
    eng = {"V": g.vector, "S": g.scalar, "T": g.tensor, "G": g, "Y": g.sync}
    clk = {k: {} for k in eng}
    cnt = {"V": 0, "S": 0, "T": 0, "G": 0}
    acc = {}
    banks = {}

    def v(name, a=0, b=None, st=1):
        buf, off, w = WHERE[name]
        return (buf, off + a, off + (w if b is None else b), st)

    def ap(x):
        return T[x[0]][:, x[1]:x[2]] if x[3] == 1 else T[x[0]][:, x[1]:x[2]:x[3]]

    def meet(x, y):
        if x[2] <= y[0] or y[1] <= x[1]:
            return False
        return not (x[3] == y[2] and x[3] > 1 and (x[1] - y[0]) % x[3])

    def need(qn, evs):
        best = {}
        for e in evs:
            if clk[qn].get(e[0], 0) < e[1] and (e[0] not in best or best[e[0]][1] < e[1]):
                best[e[0]] = e
        lst = list(best.values())
        keep = [e for e in lst if not any(o is not e and o[2].get(e[0], 0) >= e[1] for o in lst)]
        for e in keep:
            eng[qn].wait_ge(T.sem[e[0]], e[1])
        for e in keep:
            for k, x in list(e[2].items()) + [(e[0], e[1])]:
                if clk[qn].get(k, 0) < x:
                    clk[qn][k] = x

    def deps(qn, reads, writes):
        evs = []
        for lst, wr in ((reads, False), (writes, True)):
            for x in lst:
                evs += [e for k, e in banks.get(x[0], {}).items() if k != qn]
                for y in acc.get(x[0], []):
                    if meet(x, y) and (y[3] or wr) and not qn == y[4] == "T":
                        evs.append(y[5])
        return evs

    def note(qn, reads, writes, ev):
        for lst, wr in ((reads, False), (writes, True)):
            for x in lst:
                if x[0].startswith("ps"):
                    banks.setdefault(x[0], {})[qn] = ev
                l = acc.setdefault(x[0], [])
                if wr and x[3] == 1:
                    l[:] = [y for y in l if not (x[1] <= y[0] and y[1] <= x[2])]
                elif not wr:
                    l[:] = [y for y in l if not (y[:3] == x[1:] and not y[3] and y[4] == qn)]
                l.append((x[1], x[2], x[3], wr, qn, ev))

    def op(qn, fn, reads, writes):
        need(qn, deps(qn, reads, writes))
        cnt[qn] += 1
        fn().then_inc(T.sem["q" + qn], 1)
        note(qn, reads, writes, ("q" + qn, cnt[qn], dict(clk[qn])))

    def dma(qn, out, in_, sem, reads=(), writes=()):
        need(qn, deps(qn, reads, writes))
        eng[qn].dma_start(out, in_).then_inc(T.sem[sem], 16)
        note(sem, reads, writes, (sem, 16, dict(clk[qn])))

    def tt(out, a, b, o):
        op("V", lambda: g.vector.tensor_tensor(ap(out), ap(a), ap(b), o), [a, b], [out])

    def ttg(out, win, off, b, o):
        op("V", lambda: g.vector.tensor_tensor(ap(out), ap(win).indirect(ap(off)), ap(b), o), [win, off, b], [out])

    def ts(out, a, s1, o1, s2=None, o2=None):
        rd = [a] + [s for s in (s1, s2) if isinstance(s, tuple)]
        s = [ap(x) if isinstance(x, tuple) else x for x in (s1, s2)]
        if o2 is None:
            op("V", lambda: g.vector.tensor_scalar(ap(out), ap(a), s[0], None, o1), rd, [out])
        else:
            op("V", lambda: g.vector.tensor_scalar(ap(out), ap(a), s[0], s[1], o1, o2), rd, [out])

    def cp(out, a):
        op("V", lambda: g.vector.tensor_copy(ap(out), ap(a)), [a], [out])

    def cpg(out, win, off):
        op("V", lambda: g.vector.tensor_copy(ap(out), ap(win).indirect(ap(off))), [win, off], [out])

    def scat(win, off, a):
        op("V", lambda: g.vector.tensor_copy(ap(win).indirect(ap(off)), ap(a)), [off, a], [win])

    def fill(out, c):
        op("V", lambda: g.vector.memset(ap(out), c), [], [out])

    def act(out, a, fn, off=None, **kw):
        if off is None:
            op("S", lambda: g.scalar.activation(ap(out), ap(a), fn, **kw), [a], [out])
        else:
            op("S", lambda: g.scalar.activation(ap(out), ap(a).indirect(ap(off)), fn, **kw), [a, off], [out])

    def mm(out, l, r, start, stop):
        op("T", lambda: g.tensor.matmul(ap(out), ap(l), ap(r), start, stop), [l, r], [out])

    def B(name, j, w=128):
        return v(name, w * j, w * j + w)

    dma("Y", T.n0i[:, :], T.n0[:, :], "ldn0", [], [v("n0i")])
    dma("Y", T.ACT[:, :], T.acts[:, :], "ldacts", [], [v("ACT")])
    dma("Y", T.REG[:, 0:NR], T.regs[:, :], "ldregs", [], [v("REG", 0, NR)])
    dma("S", T.XR[:, :], T.rch[:, :], "ldrch", [], [v("XR")])
    fill(v("VI"), 0)
    need("S", [("qV", cnt["V"], {})])
    for t in range(RO):
        for e, row in ((1, 6), (2, 2), (3, 4)):
            c = (t * 3 + e - 1) * 256
            g.scalar.dma_start(T.VI[row::16, t * 256:t * 256 + 256], T.dr[:, c:c + 256]).then_inc(T.sem["lddr"], 16)
    ldr = ("lddr", 96, dict(clk["S"]))
    note("lddr", [], [v("VI")], ldr)
    need("Y", [ldr])
    dma("Y", T.PAYT[:, :], T.pay[:, :], "ldpay", [], [v("PAYT")])

    def iota(name, pattern, cm, **kw):
        op("G", lambda: g.iota(ap(v(name)), pattern, 0, cm, **kw), [], [v(name)])

    def aff(out, a, pattern, cmp, fillv, base, cm):
        op("G", lambda: g.affine_select(ap(out), ap(a), pattern, cmp, fillv, base, cm), [a], [out])
    some = {"allow_small_or_imprecise_dtypes": True}
    iota("KBr", [[0, 8], [1, 16]], 0, **some)
    aff(v("KBa"), v("KBr"), [[-16, 8], [0, 16]], A.is_ge, -100.0, 0, 1)
    aff(v("KB"), v("KBa"), [[16, 8], [0, 16]], A.is_ge, -100.0, 15, -1)
    iota("pI", [[0, 8]], 1)
    iota("JI", [[1, 16]], 0, **some)
    iota("LM", [[0, 16], [1, 16]], 0, **some)
    fill(v("ONES"), 1.0)
    fill(v("ZF"), 0.0)
    fill(v("ZB"), 0.0)
    for d in range(N):
        fill(v("W", 512 * d, 512 * d + 64), 0.0)
    ts(v("pA"), v("pI"), 15, A.bitwise_and)
    pc = [v("pc", i, i + 1) for i in range(12)]
    cp(pc[0], v("pA", 0, 1))
    cp(v("JU"), v("JI"))
    for i, m, a in ((1, 1, 1), (2, 1, -7), (3, 1, -8), (4, -256, 1), (5, 16, -2032), (9, 16, -2034), (10, 16, -2035), (6, 1, 4096)):
        ts(pc[i], pc[0], float(m), A.mult, float(a), A.add)
    KB, JI = v("KB"), v("JI")
    ts(v("I16"), JI, pc[0], A.is_equal)
    ts(v("BO"), KB, 0.0, A.is_ge)
    ts(v("t6"), KB, 15.0, A.is_equal)
    ts(pc[7], v("I16", 0, 1), 64.0, A.mult, v("I16", 1, 2), A.add)
    tt(pc[8], v("I16", 7, 8), v("I16", 15, 16), A.add)
    ts(pc[11], v("I16", 0, 1), 64.0, A.mult)
    tt(v("BOx"), v("BO"), v("t6"), A.subtract)
    ts(v("BOw"), v("BO"), pc[7], A.mult)
    for k in range(16):
        aff(B("LC", k), v("BOx") if k < 8 else v("BO"), [[0, 8], [1, 16]], A.is_ge, 0.0, -k, 0)
    for j in range(16):
        aff(B("LP", j), v("BOw"), [[0, 8], [1, 16]], A.is_equal, 0.0, -j, 0)
    for j in range(1, 16):
        aff(B("LT", j), v("BO"), [[16, 8], [0, 16]], A.is_ge, 0.0, j - 1, -1)
    ts(v("EM"), v("BO"), pc[8], A.mult)
    ts(v("MSK"), v("LM"), pc[0], A.is_equal, -1.0, A.mult)
    ts(v("TRASH"), JI, 16.0, A.mult, pc[6], A.add)
    for lev, i in ((1, 5), (2, 9), (3, 10)):
        ts(B("ADDK", lev - 1, 16), JI, 256.0, A.mult, pc[i], A.add)
    ts(v("BOn"), KB, 0.0, A.is_ge, -1.0, A.mult)
    for i, r in enumerate((6, 2, 4)):
        ts(B("RV", i), v("BO"), v("I16", r, r + 1), A.mult)
    for i, r in enumerate((6, 3, 5)):
        ts(B("RW", i), v("BO"), v("I16", r, r + 1), A.mult, ETA, A.mult)
    ts(v("CWa"), KB, 0.5, A.add, -ETA, A.mult)
    ts(v("m8"), v("t6"), -16384.0, A.mult)
    ts(v("t5"), v("BO"), v("I16", 0, 1), A.mult)
    tt(v("CWb"), v("CWa"), v("m8"), A.add)
    ts(v("t1"), KB, pc[1], A.is_equal)
    ts(v("t2"), KB, pc[0], A.is_equal)
    ts(v("t3"), KB, pc[2], A.is_equal)
    ts(v("t4"), KB, pc[3], A.is_equal)
    tt(v("CW"), v("CWb"), v("t5"), A.mult)
    tt(v("D"), v("t1"), v("t2"), A.subtract)
    tt(v("d2a"), v("t1"), v("t2"), A.subtract)
    tt(v("d2b"), v("t3"), v("t4"), A.subtract)
    ts(v("m8"), KB, 8.0, A.is_lt)
    tt(v("d2c"), v("d2a"), v("d2b"), A.add)
    cp(v("NU0"), v("n0i"))
    cp(v("IDh"), v("t2"))
    ts(v("ID13"), v("t2"), 13.0, A.mult)
    tt(v("D2"), v("d2c"), v("m8"), A.mult)
    cp(v("IDb"), v("t2"))
    cp(v("SHb"), v("t1"))
    for j in range(2):
        ts(B("SelNb", j), KB, float(j), A.is_equal, -1.0, A.mult)
    ts(v("nA"), v("n0i"), 13.0, A.mult, 1.0, A.add)
    for h in range(2):
        cpg(B("A1", h), v("ACT"), B("NU0", h, 8))
    for j in range(16):
        ts(B("SelN", j), KB, float(j), A.is_equal, -1.0, A.mult)
    ts(v("nB"), v("nA"), ND - 1, A.bitwise_and)
    ts(v("G5"), v("A1"), 5.0, A.mult)
    ts(v("nC"), v("nB"), 6, A.logical_shift_right)
    ts(v("nD"), v("nB"), 63, A.bitwise_and)
    ts(v("bhI"), v("G5"), 6, A.logical_shift_right, 31, A.bitwise_and)
    ts(v("Nh"), v("nC"), 64.0, A.add)
    cp(v("Nl"), v("nD"))
    ts(v("blI"), v("G5"), 63, A.bitwise_and)
    cp(v("bh"), v("bhI"))
    ttg(v("NMXh"), v("Nh"), v("JU"), v("MSK"), A.mult)
    ttg(v("NMXl"), v("Nl"), v("JU"), v("MSK"), A.mult)
    cp(v("bl"), v("blI"))
    cp(v("ps0", 256, 512), v("XR"))
    ts(v("T5"), v("ACT"), 5.0, A.mult)
    ts(v("VI15"), v("VI"), 15, A.bitwise_and)
    cp(v("HPv", 0, 256), v("VI", 0, 256))
    ts(v("HPv", 256, 512), v("VI", 256, 512), pc[11], A.add)
    cp(v("HP15"), v("VI15"))

    def Cb(p):
        return v("ps%d" % (1 + p), 0, 128)

    def Mb(p, a, b):
        return v("ps%d" % (3 + p), a, b)

    recs = v("REG", 0, NR)
    todo = []

    def gap(n):
        while n > 0 and todo:
            todo.pop(0)()
            n -= 1

    def minima(p, x, lev, draws15):
        def one(k):
            mk = B("MN", 16 * p + k)
            tt(mk, v("P", 2048 * p + k, 2048 * p + 2048, 16), x, A.min)
            if k == 0:
                mm(Mb(p, 0, 128), v("CW"), v("ONES"), True, False)
                mm(Mb(p, 0, 128), B("RW", lev - 1), draws15, False, False)
            mm(Cb(p), B("LC", k), mk, k == 0, k == 15)
        return [lambda k=k: one(k) for k in range(16)]

    def cond(p):
        return B("Q", 2 * p + 1)

    def decide(p, v1, n):
        cp(B("CM", p), Cb(p))
        mm(Mb(p, 0, 128), v("EM"), B("CM", p), False, True)
        gap(n)
        tt(B("Tt", p), Mb(p, 0, 128), v1, A.mult)
        gap(n)
        tt(cond(p), Cb(p), B("Tt", p), A.is_gt)

    def listed(out, name, a, b, more=False):
        for j in range(16):
            mm(out, B("SelN", j), v(name, a + j, b, 16), j == 0, j == 15 and not more)

    def chosen(p, lists):
        act(B("Pk", p), B("P", p, 2048), F.Identity, off=lists, bias=1.0)

    def thresholds(out, ps):
        act(out, ps, F.Identity, scale=1.0 / 64, bias=DEL / 64)

    sent = {"locH": 0, "locZ": 0}
    plans = [plan(r, cores, topo) for r in range(N)]
    mine = q // 4
    order = (mine, 1 - mine)

    def send(src, dst, width, swidth, call, sem, loc):
        tr = []
        for r, e in plans[q][call]:
            rid, pid, _ = topo.addr(cores[r])
            tr.append(RemoteDMATransfer(dst_ids=[DstId(rid=rid, pnc=pid)], dma_engine_mask=sum(1 << x for x in e), remote_sem=T.sem[sem],
                                        srcs=[T[src][:, r * swidth:r * swidth + width]], dsts=[T[dst][:, q * width:q * width + width]]))
            sent[loc] += len(e)
        g.remote_dma_fused(tr, local_sem=T.sem[loc])

    def landed(buf, width, sems):
        for i, h in enumerate(order):
            val = sum(len(e) for r in range(N) if r != q for d, e in plans[r][i] if d == q)
            for r in range(4 * h, 4 * h + 4):
                if r != q:
                    note(sems[i], [], [B(buf, r, width)], (sems[i], val, {}))

    def key_sums(p):
        mm(B("ps7", 1 + p), v("BOn"), B("Q", 2 * p), True, True)
        listed(B("ps7", p, 8), "Q", 256 * p, 256 * p + 128)

    def keys(h, live):
        kl, KMh, KLh, dd = B("ps7", h, 8), B("KM", h, 8), B("KL", h, 8), B("dead", h, 8)
        lv = B(live, h, 8)
        return [lambda: ts(dd, lv, -9999.0, A.mult, 9999.0, A.add), lambda: cp(B("KBs", h), B("ps7", 1 + h)), lambda: tt(KMh, kl, lv, A.mult),
                lambda: ts(B("KI", h, 8), kl, 2048.0, A.add), lambda: tt(KLh, KMh, dd, A.add)]

    def matches(c, a, b):
        e = lambda x: 240 * c + x
        ts(v("E", e(a), e(b)), v("KBs", a, b), v("KL", c, c + 1), A.is_equal)
        a = max(a, 16 * c + 16)
        if a < b:
            mm(v("ps6", 256 + a, 256 + b), v("BO"), v("E", e(a), e(b)), False, False)

    def inner(h):
        return [lambda c=c: matches(c, 16 * c, 128 * h + 128) for c in range(8 * h, 8 * h + 8)]

    def across():
        return [lambda c=c: matches(c, 128, 256) for c in range(8)]

    def open_sums():
        mm(v("ps6", 256, 512), v("BO"), v("ZB"), True, False)

    def finish_sums(i, live):
        for j in range(1, 16):
            mm(v("ps6", 256 + j, 512, 16), B("LT", j), v("E", j, 4096, 256), False, j == 15)
        ai = B("AI", i, 16)
        ts(v("KJ"), v("KI"), 3277.0, A.mult)
        ts(ai, v("KJ"), NR - 1, A.bitwise_and)
        cp(B("AU", i, 16), ai)
        tt(v("w3"), ai, v("TRASH"), A.subtract)
        tt(v("w4"), v("w3"), v(live), A.mult)

    def winners(i):
        def one():
            cp(v("DPs"), v("ps6", 256, 512))
            listed(v("ps7", 32, 48), "DPs", 0, 256)
        return [one, lambda: ts(v("w1"), v("ps7", 32, 48), 0.0, A.is_equal), lambda: tt(v("w2"), v("w1"), v("w4"), A.mult),
                lambda: tt(v("w5"), v("w2"), v("TRASH"), A.add), lambda: cp(B("OW", i, 16), v("w5"))]

    def change(win, off, other, o, i):
        ttg(v("NEW"), win, off, other, o)
        ts(v("NEWc"), v("NEW"), 15.0, A.min, -15.0, A.max)
        scat(v("REG"), B("OW", i, 16), v("NEWc"))

    for t in range(RO):
        LAND, NZ, ZL = "LAND%d" % t, "NZ%d" % t, "ZL%d" % t

        def places(p):
            decide(p, B("V1", p), 1)
            oh, ohd, lst = Mb(p, 128, 256), Mb(p, 256, 384), Mb(p, 384, 400)
            mm(ohd, v("D2"), cond(p), True, True)
            mm(oh, v("D"), cond(p), True, True)
            gap(2)
            init = pc[4] if p == 0 else v("CNT", 127, 128)
            op("V", lambda: g.vector.tensor_tensor_scan(ap(B("CNT", p)), ap(ohd), ap(v("ZF")), ap(init), A.add, A.add), [ohd, v("ZF"), init], [B("CNT", p)])
            tt(B("ph", p), oh, B("bh", p), A.mult)
            tt(B("Q", 2 * p), ohd, B("CNT", p), A.mult)
            tt(B("pl", p), oh, B("bl", p), A.mult)
            listed(lst, "Q", 256 * p, 256 * p + 256, True)
            mm(Mb(p, 392, 400), v("IDh"), v("ADDK", 0, 8), False, True)
            o = B("ps5", 2 + p)
            mm(o, v("IDb"), B("HPv", 2 * t + p), True, False)
            mm(o, v("SHb"), B("HP15", 2 * t + p), False, False)
            for name, i in (("NMXh", 0), ("NMXl", 1), ("ph", 0), ("pl", 1)):
                mm(o, B("SelNb", i), B(name, p), False, name == "pl")
            gap(6)
            ts(B("KU", p, 8), Mb(p, 392, 400), 2048.0, A.add)
            ts(B("SL", 2 * p + 1, 8), Mb(p, 384, 392), -2.0, A.mult, 1.0, A.add)
            ts(B("SL", 2 * p, 8), Mb(p, 384, 392), -2.0, A.mult)
            chosen(p, B("KU", p, 8))
            act(B("SC", 2 * p + 1), o, F.Copy)

        def xpay(p):
            tt(B("SC", 2 * p), B("ps0", 2 + p), B("Pk", p), A.min)

        act(v("P", 0, 1024), recs, F.Relu, off=v("A1", 0, 64))
        op("V", lambda: g.vector.tensor_scalar(ap(v("P", 1024, 2048)), ap(recs).indirect(ap(v("A1", 64, 128))), 0.0, None, A.max),
           [recs, v("A1", 64, 128)], [v("P", 1024, 2048)])
        act(B("P", 1, 2048), recs, F.Relu, off=B("A1", 1))
        mm(v("ps5", 0, 256), B("RV", 0), B("HPv", t, 256), True, True)
        thresholds(v("V1", 0, 256), v("ps5", 0, 256))
        todo += minima(0, B("ps0", 2), 1, B("HP15", 2 * t))
        gap(16)
        if t:
            need("V", [("locH", sent["locH"], {})])
        todo += minima(1, B("ps0", 3), 1, B("HP15", 2 * t + 1))
        places(0)
        gap(99)
        todo += [lambda: xpay(0), lambda: scat(v("W"), B("SL", 0, 16), B("SC", 0, 256))]
        places(1)
        gap(99)
        scat(v("W"), B("SL", 3, 8), B("SC", 3))
        xpay(1)
        scat(v("W"), B("SL", 2, 8), B("SC", 2))
        need("G", deps("G", [v("W")], []))
        for i in range(2):
            send("W", LAND, 64, 512, i, "h%s%d" % ("AB"[i], t), "locH")
        if t == 0:
            ts(v("G12"), v("G5"), 4095, A.bitwise_and)
            ts(v("Bg1"), v("G12"), -2048.0, A.add)
        for p in range(2):
            tt(B("Q", 2 * p), Mb(p, 128, 256), B("Bg1", p), A.mult)
            key_sums(p)
        cp(B(LAND, q, 64), v("W", 512 * q, 512 * q + 64))
        for p in range(2):
            ts(B("OFF", p, 8), Mb(p, 384, 392), -1.0, A.mult)
        open_sums()
        ts(v("oc"), v("OFF"), 255, A.bitwise_and)
        ts(v("oa"), v("OFF"), 8, A.logical_shift_right)
        ts(v("GO"), v("oc"), 32.0, A.is_lt)
        ts(v("ob"), v("OFF"), 31, A.bitwise_and)
        ts(v("od"), v("oa"), 32.0, A.mult)
        todo += [f for two in zip(keys(0, "GO"), keys(1, "GO")) for f in two] + [lambda c=c: matches(c, 16 * c, 256) for c in range(16)]
        gap(99)
        tt(v("oe"), v("od"), v("ob"), A.add)
        finish_sums(0, "GO")
        cp(v("ZIX"), v("oe"))
        if t == 0:
            ts(v("T12"), v("T5"), 4095, A.bitwise_and)
            ts(v("ZMa"), v("t2"), 16.0, A.mult)

        landed(LAND, 64, ("hA%d" % t, "hB%d" % t))

        def gathers(p, off):
            cpg(B("A16", p), v("ACT"), off)
            act(B("P", p, 2048), recs, F.Relu, off=B("A16", p))

        def more(p, off):
            act(B("Bg", p), v("BT"), F.Copy, off=off)

        def receive(h, ps):
            o = v("ps7", 48 + 8 * h, 56 + 8 * h)
            for j in range(16):
                mm(o, B("LP", j), v(LAND, 256 * h + 2 * j + 1, 256 * h + 256, 32), j == 0, j == 15)
            ni, nn, lu = B("NI", h, 8), B("NN", h, 8), B("LU", h, 8)
            cp(ni, o)
            ts(nn, ni, ND - 1, A.bitwise_and)
            cp(lu, nn)
            cpg(B("A16", h), v("ACT"), lu)
            for i in (0, 1):
                mm(B(ps, i), B("RV", 1 + i), v(LAND, 256 * h + 1, 256 * h + 256, 2), True, True)
            act(B("P", h, 2048), recs, F.Relu, off=B("A16", h))
            thresholds(B("V1", h, 256), v(ps, 0, 256))
            cp(B("ps0", h), v(LAND, 256 * h, 256 * h + 256, 2))
            cp(B("NF", h, 8), nn)
            ts(B("LIVE", h, 8), ni, 4096.0 * (t + 1), A.is_ge)

        def minima23(p, lev):
            return minima(p, B("ps0", p), lev, v(LAND, 256 * p + 1, 256 * p + 256, 2))

        def far(p, lev, n):
            decide(p, B("V1", 2 * p + lev - 2), n[0])
            mm(Mb(p, 128, 256), v("D"), cond(p), True, True)
            gap(n[1])
            tt(B("Q", 2 * p), Mb(p, 128, 256), B("Bg", p), A.mult)
            listed(Mb(p, 384, 400), "Q", 256 * p, 256 * p + 256, True)
            mm(Mb(p, 384, 392), v("ID13"), B("NF", p, 8), False, False)
            mm(Mb(p, 392, 400), v("IDh"), v("ADDK", 16 * lev - 16, 16 * lev - 8), False, True)
            if lev == 3:
                key_sums(p)
            gap(n[2])
            ts(B("LI", p, 16), Mb(p, 384, 400), 2048.0 + lev, A.add)
            gap(n[3])
            ts(B("L2", p, 16), B("LI", p, 16), ND - 1, A.bitwise_and)
            gap(n[3])
            b = 16 + 32 * (lev - 2) + 16 * p
            cp(v("LU", b, b + 16), B("L2", p, 16))
            if lev == 2:
                cpg(B("A16", p), v("ACT"), v("LU", b, b + 8))
            chosen(p, v("LU", b + 8, b + 16))
            if lev == 2:
                act(B("P", p, 2048), recs, F.Relu, off=B("A16", p))
                more(p, v("LU", b, b + 8))
                cp(B("NF", p, 8), B("L2", 2 * p, 8))
                gap(n[4])
                tt(B("ps0", p), B("ps0", p), B("Pk", p), A.min)

        def leaf(p):
            tt(B("XS", p), B("ps0", p), B("Pk", p), A.min)
            ttg(B("VAL", p), v("PAYT"), v("LU", 48 + 16 * p, 56 + 16 * p), B("XS", p), A.min)
            mm(Cb(p), v("ZM"), B("VAL", p), True, True)
            act(B(NZ, p), Cb(p), F.Sign, scale=-1.0)
            i = int(p != mine)
            need("G", deps("G", [B(NZ, p)], []))
            send(NZ, ZL, 32, 32, i, "z%s%d" % ("AB"[i], t), "locZ")

        a, b = order
        receive(a, "ps5")
        todo += winners(0)
        gap(2)
        receive(b, "ps6")
        gap(99)
        if t == 0:
            ts(v("BT"), v("T12"), -2048.0, A.add)
            tt(v("ZM"), v("ZMa"), v("BO"), A.subtract)
        for p in order:
            more(p, B("LU", p, 8))
        todo += minima23(a, 2)
        gap(16)
        todo += minima23(b, 2)
        far(a, 2, (0, 0, 5, 1, 2))
        gap(99)
        far(b, 2, (0, 0, 0, 0, 0))
        todo += minima23(a, 3)
        gap(16)
        todo += minima23(b, 3)
        far(a, 3, (0, 0, 5, 1, 0))
        gap(99)
        leaf(a)
        todo += [open_sums] + keys(a, "LIVE") + inner(a)
        far(b, 3, (2, 2, 6, 1, 0))
        leaf(b)
        gap(99)

        todo += keys(b, "LIVE") + inner(b) + across()
        gap(99)
        finish_sums(1, "LIVE")
        cp(B(ZL, q, 32), B(NZ, q, 32))
        todo += winners(1)
        gap(99)
        change(recs, B("AU", 1, 16), v(NZ), A.subtract, 1)
        cpg(v("OLD"), recs, B("AU", 0, 16))
        landed(ZL, 32, ("zA%d" % t, "zB%d" % t))
        change(v(ZL), v("ZIX"), v("OLD"), A.add, 0)

    dma("Y", T.yr[:, :], T.REG[:, 0:NR], "st", [recs], [])
    g.sync.wait_ge(T.sem.st, 16)
    for k in "VSTG":
        need("Y", [("q" + k, cnt[k], {})])
    for k in sent:
        g.wait_ge(T.sem[k], sent[k])
